import numpy as np, ml_dtypes
CORES = [40,41,42,43,44,45,46,47]
N = 8
import mx_ref
BF = ml_dtypes.bfloat16
def pick(q, e):
    c = np.concatenate([q[0].reshape(128, -1, 4), np.zeros((128, 1, 4), np.uint8)], axis=1); s = np.concatenate([q[1], np.ones((16, 1), np.uint8)], axis=1)
    return (np.ascontiguousarray(c[:, e].reshape(128, -1)), np.ascontiguousarray(s[:, e]))
def join(*qs):
    return (np.concatenate([q[0] for q in qs], axis=1), np.concatenate([q[1] for q in qs], axis=1))
def put(q, e, v):
    c, s = q[0].reshape(128, -1, 4).copy(), q[1].copy(); c[:, e] = v[0].reshape(128, -1, 4); s[:, e] = v[1]
    return (c.reshape(128, -1), s)
def pk(c, s):
    return (np.ascontiguousarray(c), mx_ref.live(s))
def emit(q):
    return q[0], q[1]
def decode(q):
    o = []
    for b in range(4):
        e = np.zeros((128, 128, 4), np.float32); e[np.arange(128), np.arange(128), b] = 1
        o.append(mx_ref.matmul(mx_ref.quantize(e.reshape(128, 512).astype(BF)), q))
    return np.stack(o, axis=2).reshape(128, -1)
def f(rng, *shape):
    return mx_ref.flush((rng.standard_normal(shape, dtype=np.float32) * np.exp2(rng.integers(-2, 3, shape[:-1] + (1,)))).astype(BF))
def wide(rng, *shape, cols=0):
    v = rng.standard_normal(shape, dtype=np.float32) * np.exp2(rng.integers(-12, 13, shape)).astype(np.float32)
    if cols: v *= np.repeat(np.exp2(rng.integers(-cols, cols + 1, shape[:-2] + (1, shape[-1] // 4))) * (rng.random(shape[:-2] + (1, shape[-1] // 4)) > 0.0625), 4, axis=-1).astype(np.float32)
    return mx_ref.flush(v.astype(BF))
T, CAPP = 128, 32
def quads(q, e):
    c = np.concatenate([q[0].reshape(128, -1, 4), np.zeros((128, 1, 4), np.uint8)], axis=1); s = np.concatenate([q[1], np.ones((16, 1), np.uint8)], axis=1)
    return (np.concatenate([c[32 * h:32 * h + 32][:, e[h]] for h in range(4)]).reshape(128, -1), np.concatenate([s[4 * h:4 * h + 4][:, e[h]] for h in range(4)]))
def level(b, z):
    n, e = z[1].shape[1], []
    for h in range(4):
        only = np.where(np.arange(4)[:, None] == h, np.arange(n)[None, :], -1)
        e.append(np.argmax(mx_ref.matmul(b, quads(z, only)) + np.float32(0), axis=0))
    e = np.stack(e)
    return e, quads(b, e)
def big(v):
    v = v.astype(np.float32)
    v[np.abs(v) < np.float32(2.0 ** -16)] = 0
    return v.astype(BF)
def coarse(v):
    v = v.copy()
    v[:, N:] = 0
    return np.stack([v.reshape(128, 512)] * N)
def planted(rng, cell, low=False):
    at = rng.permutation(N)[np.arange(128) // (128 // N)]
    c = (1 + rng.random((128, 128, 4))) * (at[:, None] == np.arange(128)[None, :])[:, :, None]
    on = at[None, :, None] == cell[:, None, :]
    v = np.where(on[:, :, :, None], 8 + 8 * rng.random((N, 128, T, 4)), 2 * rng.random((N, 128, T, 4)) - 1)
    if low:
        u = 1 + rng.random((N, 128, T // 2, 4))
        v[:, :, 1::2] = np.where(on[:, :, 1::2, None], -0.5 * u, -8 * u)
        c = c * 2.0 ** 20
    v = v * np.exp2(rng.integers(-3, 4, (N, 1, T, 1)))
    return {"x": big(v.reshape(N, 128, 4 * T)), "co": coarse(big(c))}
def setup_inputs(rng):
    return {"x": big(f(rng, N, 128, 4 * T)), "co": coarse(big(f(rng, 128, 512)).reshape(128, 128, 4)), "b1": big(f(rng, N, 128, 512)), "b2": big(f(rng, N, 128, 512)), "w": f(rng, N, 128, 512)}
def setup_inputs_spread(rng):
    d = setup_inputs(rng)
    d["x"], d["b1"] = big(wide(rng, N, 128, 4 * T, cols=6)), big(wide(rng, N, 128, 512))
    return d
def setup_inputs_ties(rng):
    d = setup_inputs(rng)
    for k in ("b1", "b2"):
        b = d[k].reshape(N, 128, 128, 4).copy()
        for r in range(N):
            for h in range(4): b[r, 32 * h:32 * h + 32] = b[r, 32 * h:32 * h + 32][:, rng.permutation(128) % 32]
        d[k] = b.reshape(N, 128, 512)
    c = d["co"][0].reshape(128, 128, 4).copy()
    c[:, :N] = c[:, rng.permutation(N) % (N // 2)]
    d["co"] = coarse(c)
    return d
def setup_inputs_crowd(rng):
    g, cell = int(rng.integers(0, N)), []
    for s in range(N):
        o = rng.permutation(np.delete(np.arange(N), g))
        if o[0] == s: o = o[::-1]
        m = int(rng.integers(1, 17))
        cell.append(rng.permutation(np.concatenate([np.full(CAPP + m, g), np.full(CAPP, o[0]), o[1:][rng.integers(0, N - 2, T - 2 * CAPP - m)]])))
    return {**setup_inputs(rng), **planted(rng, np.stack(cell))}
def setup_inputs_few(rng):
    g, a, b = [int(i) for i in rng.permutation(N)[:3]]
    cell = np.delete(np.arange(N), g)[rng.integers(0, N - 1, (N, T))]
    cell[a], cell[b] = a, a
    return {**setup_inputs(rng), **planted(rng, cell, low=True)}
def setup_inputs_zero(rng):
    d, h = setup_inputs(rng), [int(i) for i in rng.permutation(4)]
    neg, pat, gap = [slice(32 * i, 32 * i + 32) for i in h[:3]]
    p = (1 + rng.random((32, 1, 4))) * np.exp2(rng.integers(-2, 3, (32, 1, 1)))
    v, b, c = d["x"].astype(np.float32).reshape(N, 128, T, 4), d["b1"].astype(np.float32).reshape(N, 128, 128, 4), d["co"][0].reshape(128, 128, 4).copy()
    u = d["b2"].astype(np.float32)
    c[neg], c[pat] = 0, 0
    c[:, int(rng.integers(0, N))] = 0
    v[:, neg], b[:, neg], u[:, neg] = -np.abs(v[:, neg]), np.abs(b[:, neg]), np.abs(u[:, neg])
    v[:, pat] = p
    for r in range(N):
        e, k = rng.permutation(T), rng.integers(0, 4, 128)
        v[r, gap][:, e[T // 8:T // 2]] = 0
        v[r][:, e[:T // 8]] = 0
        k[int(rng.integers(0, 128))] = 0
        b[r, pat] = p * np.exp2(-k.astype(np.float64))[:, None]
        if r % 2 == 0: b[r, neg, int(rng.integers(0, 128))] = 0
    k = np.float32(2.0 ** 20)
    d["x"], d["b1"], d["b2"], d["co"] = big(v.reshape(N, 128, 4 * T) * k), big(b.reshape(N, 128, 512) * k), big(u * k), coarse(c)
    return d
def check_inputs(d):
    b = []
    for k in ("x", "co", "b1", "b2", "w"):
        v = np.abs(d[k].astype(np.float32))
        if not (np.isfinite(v).all() and ((v == 0) | (v >= 2.0 ** -30) & (v <= 2.0 ** 30)).all()): b.append("a value of " + k)
    c = d["co"].astype(np.float32)
    if (c[:, :, 4 * N:] != 0).any(): b.append("co has numbers behind its first N columns")
    if (c != c[:1]).any(): b.append("co isn't the same on all ranks")
    return b
def reference(x, co, b1, b2, w):
    oc, osc = np.zeros((N, 128, 8 * T), np.uint8), np.zeros((N, 16, 2 * T), np.uint8)
    wn, y = np.full((N, 8, T), -1, np.float32), np.zeros((N, 128, T), np.float32)
    q = [mx_ref.quantize(x[s]) for s in range(N)]
    taken = np.full((N, N, CAPP), -1)
    for s in range(N):
        cell = np.argmax(mx_ref.matmul(mx_ref.quantize(co[s]), q[s])[:N] + np.float32(0), axis=0)
        for d in range(N):
            t = np.flatnonzero(cell == d)[:CAPP]
            taken[s, d, :len(t)] = t
    home = [pick(q[s], np.full(2 * T, -1)) for s in range(N)]
    for d in range(N):
        z = join(*[pick(q[s], taken[s, d]) for s in range(N)])
        n1, v1 = level(mx_ref.quantize(b1[d]), z)
        r = mx_ref.quantize((decode(z) - decode(v1)).astype(BF))
        n2, v2 = level(mx_ref.quantize(b2[d]), r)
        for s in range(N):
            k = np.flatnonzero(taken[s, d] >= 0)
            t, i = taken[s, d][k], s * CAPP + k
            wn[s, :4, t], wn[s, 4:, t] = n1[:, i].T, n2[:, i].T
            home[s] = put(put(home[s], t, pick(v1, i)), T + t, pick(v2, i))
    for s in range(N):
        oc[s], osc[s] = emit(home[s])
        m = mx_ref.matmul(mx_ref.quantize(w[s]), home[s])
        y[s] = m[:, :T] + m[:, T:]
    return {"oc": oc, "osc": osc, "wn": wn, "y": y}

@@ -1,0 +1,324 @@
+from concourse.bass import DstId, RemoteDMATransfer
+from concourse.mybir import dt, AluOpType, AxisListType, ActivationFunctionType
+
+BF, F32, I32, U16, COD, PL = "bfloat16", "float32", "int32", "uint16", "float8_e4m3fn_x4", "uint8"
+SCRATCH = {
+    "xt": ("sbuf", [128, 512], BF), "cot": ("sbuf", [128, 512], BF), "wt": ("sbuf", [128, 512], BF),
+    "bt1": ("sbuf", [128, 2048], BF), "bt2": ("sbuf", [128, 2048], BF),
+    "et": ("sbuf", [128, 2048], BF), "en": ("sbuf", [128, 2048], BF),
+    "trt": ("sbuf", [128, 512], BF), "ct": ("sbuf", [128, 512], BF), "mt": ("sbuf", [128, 512], BF),
+    "rqt": ("sbuf", [128, 576], BF), "ht": ("sbuf", [128, 512], BF), "zt": ("sbuf", [128, 512], BF),
+    "rt": ("sbuf", [128, 1024], BF),
+    "ones": ("sbuf", [128, 128], BF), "ident": ("sbuf", [128, 128], BF), "tri": ("sbuf", [128, 128], BF),
+    "neg": ("sbuf", [128, 128], F32), "c75": ("sbuf", [128, 8], BF), "c128": ("sbuf", [128, 8], BF),
+    "ri": ("sbuf", [128, 128], BF), "qrow": ("sbuf", [128, 16], F32), "nrow": ("sbuf", [128, 16], F32),
+    "crow": ("sbuf", [128, 8], F32), "pi": ("sbuf", [128, 4], I32), "pj": ("sbuf", [128, 16], I32),
+    "pc": ("sbuf", [128, 16], F32), "lo75": ("sbuf", [128, 4], F32), "qoff": ("sbuf", [128, 4], F32), "mask8": ("sbuf", [128, 8], F32),
+    "rmc": ("sbuf", [128, 8], F32), "val": ("sbuf", [128, 4], F32), "s16": ("sbuf", [128, 4], F32),
+    "qone": ("sbuf", [128, 16], F32), "qa": ("sbuf", [128, 16], F32), "ha": ("sbuf", [128, 4], F32), "hb": ("sbuf", [128, 4], F32),
+    "hk": ("sbuf", [128, 4], F32), "hr": ("sbuf", [128, 4], F32), "hrr": ("sbuf", [128, 4], F32),
+    "loff": ("sbuf", [128, 16], U16), "hoff": ("sbuf", [128, 8], U16),
+    "rm1": ("sbuf", [128, 1024], F32), "rm2": ("sbuf", [128, 1024], F32), "sg1": ("sbuf", [128, 1024], BF), "sg2": ("sbuf", [128, 1024], BF),
+    "n1": ("sbuf", [128, 8], F32), "n2": ("sbuf", [128, 8], F32), "m1": ("sbuf", [128, 32], BF), "m2": ("sbuf", [128, 32], BF),
+    "t1": ("sbuf", [128, 32], BF), "t2": ("sbuf", [128, 32], BF), "td1": ("sbuf", [128, 64], BF), "td2": ("sbuf", [128, 64], BF),
+    "tt1": ("sbuf", [128, 64], BF), "tt2": ("sbuf", [128, 64], BF), "off1": ("sbuf", [128, 16], U16), "off2": ("sbuf", [128, 16], U16),
+    "ws1": ("dram", [8, 128, 1], BF), "ws2": ("dram", [8, 128, 1], BF), "wl1": ("dram", [8, 128, 1], BF), "wl2": ("dram", [8, 128, 1], BF),
+    "wrow": ("sbuf", [128, 272], BF), "wnf": ("sbuf", [128, 128], F32), "yt": ("sbuf", [128, 128], F32),
+}
+for _n, _w in (("x", 128), ("co", 128), ("w", 128), ("b1", 512), ("b2", 512), ("e", 512), ("ne", 512), ("tr", 128), ("c", 128),
+               ("m", 128), ("rq", 144), ("h", 128), ("slot", 256), ("land", 256), ("va", 256), ("r", 256), ("vb", 256),
+               ("hva", 384), ("hvb", 384), ("oa", 128), ("ob", 128)):
+    SCRATCH["k_" + _n] = ("sbuf", [128, _w], COD)
+    SCRATCH["s_" + _n] = ("sbuf", [128, _w], PL)
+for _n in range(8):
+    SCRATCH["p%d" % _n] = ("psum", [128, 512], F32)
+SEMAPHORES = ["cv", "cs", "ce", "cg", "dx", "dco", "db1", "db2", "dw", "dn1", "dn2", "do1", "do2", "df1", "df2", "dst",
+              "ra", "rb", "rva", "rvb", "rn1", "rn2", "loc"]
+
+ADD, SUB, MUL, MAX = AluOpType.add, AluOpType.subtract, AluOpType.mult, AluOpType.max
+GE, EQ, NE = AluOpType.is_ge, AluOpType.is_equal, AluOpType.not_equal
+AND = AluOpType.bitwise_and
+COPY, SIGN = ActivationFunctionType.Copy, ActivationFunctionType.Sign
+LOW = -1e29
+R16 = 1.5 * 2.0 ** 27
+
+
+def rank_program(g, core, T, topo):
+    me = T.rank_of(core)
+    if me is None:
+        return
+    ops, queue = [], {"v": g.vector, "s": g.scalar, "e": g.tensor, "g": g, "y": g.sync}
+    own_sem = {"v": "cv", "s": "cs", "e": "ce", "g": "cg"}
+
+    def add(q, fn, deps=(), sem=None, inc=1):
+        ops.append((q, fn, list(deps), own_sem[q] if sem is None else sem, inc))
+        return len(ops) - 1
+
+    def V(fn, *deps): return add("v", fn, deps)
+    def S(fn, *deps): return add("s", fn, deps)
+    def E(fn, *deps): return add("e", fn, deps)
+    def G(fn, *deps): return add("g", fn, deps)
+    def D(q, sem, out, in_, *deps): return add(q, lambda: queue[q].dma_start(out, in_), deps, sem, 16)
+
+    v, sc, te = g.vector, g.scalar, g.tensor
+    K = lambda n, a, b: T["k_" + n][:, a:b]
+    P = lambda n, a, b: T["s_" + n][:, a:b]
+
+    def quant(n, tile, a, b, src, *deps):
+        return V(lambda: v.quantize_mx(K(n, a, b), P(n, a, b), T[tile][:, src:src + 4 * (b - a)]), *deps)
+
+    def mm(bank, n, w, wa, x, xa, start, stop, *deps):
+        return E(lambda: te.matmul_mx(T["p%d" % bank][:, 0:n], K(w, wa, wa + 128), P(w, wa, wa + 128), K(x, xa, xa + n), P(x, xa, xa + n), start, stop), *deps)
+
+    def pick(o, a, b, w, wn, off, c, *deps):
+        k = (b - a) // 16
+        return (V(lambda: v.tensor_copy(K(o, a, b).bitcast(dt.uint32), K(w, 0, wn).bitcast(dt.uint32).indirect(T[off][:, c:c + k])), *deps),
+                S(lambda: sc.activation(P(o, a, b), P(w, 0, wn).indirect(T[off][:, c:c + k]), COPY), *deps))
+
+    others = [d for d in range(len(T.cores)) if d != me]
+    far = [d for d in others if topo.die(T.cores[d]) != topo.die(core)]
+    near = [d for d in others if d not in far]
+    eng = {}
+    for part, k in ((far, 0), (near, 1)):
+        for i, d in enumerate(part):
+            e = topo.engines(core, T.cores[d])[k::2]
+            w = len(e) // 4
+            eng[d] = e[w * i:w * i + w]
+    expect = {}
+
+    def send(src, dst, sem, one, *deps):
+        def call():
+            tr = []
+            for d in far + near:
+                rid, pid, _ = topo.addr(T.cores[d])
+                m = sum(1 << e for e in (eng[d][:1] if one else eng[d]))
+                tr.append(RemoteDMATransfer(dst_ids=[DstId(rid=rid, pnc=pid)], dma_engine_mask=m, remote_sem=T.sem[sem], src=src(d), dst=dst))
+            return g.remote_dma_fused(tr, local_sem=T.sem["loc"])
+        for d in others:
+            n = 1 if one else len(eng[d])
+            expect["loc"] = expect.get("loc", 0) + n
+        return add("g", call, deps, "")
+
+    def per(s, one):
+        c = T.cores[s]
+        return 1 if one else len(topo.engines(c, core)) // 8
+
+    def arrivals(sem, ranks, n, one):
+        expect[sem] = n * sum(per(s, one) for s in ranks if s != me)
+        return (sem, expect[sem])
+
+    dx = D("y", "dx", T.xt[:], T.x[:])
+    dco = D("s", "dco", T.cot[:, 0:32], T.co[:, 0:32])
+    ones = V(lambda: v.memset(T.ones[:], 1.0))
+    ztm = V(lambda: v.memset(T.zt[:], 0.0))
+    mtm = V(lambda: v.memset(T.mt[:], 0.0))
+    c75 = V(lambda: v.memset(T.c75[:], -7.5))
+    cot = V(lambda: v.memset(T.cot[:, 32:512], 0.0))
+    neg = V(lambda: v.memset(T.neg[:], LOW))
+
+    ga = G(lambda: g.affine_select(T.tri[:], T.ones[:], [[1, 128]], GE, 0.0, 0, -1), ones)
+    g0 = G(lambda: g.affine_select(T.trt[:, 0:512:4], T.tri[:], [[1, 128]], NE, 1024.0, 0, -1), ga)
+    g2 = G(lambda: g.affine_select(T.trt[:, 2:512:4], T.ones[:], [[0, 128]], EQ, 0.0, 0, 1), ones)
+    g3 = G(lambda: g.affine_select(T.trt[:, 3:512:4], T.ones[:], [[0, 128]], EQ, 0.0, -1, 1), ones)
+    gi = G(lambda: g.iota(T.c128[:], [[128, 8]], 0, 0, allow_small_or_imprecise_dtypes=True))
+    gm2 = G(lambda: g.affine_select(T.mt[:, 2:32:4], T.c128[:], [[0, 8]], EQ, 0.0, 0, 1), gi, mtm)
+    gm3 = G(lambda: g.affine_select(T.mt[:, 3:32:4], T.c75[:], [[0, 8]], EQ, 0.0, -1, 1), c75, mtm)
+    gp = G(lambda: g.iota(T.pi[:], [[0, 4]], 0, 1))
+    gq = G(lambda: g.iota(T.qrow[:], [[128, 8], [16, 2]], 1024, 0, allow_small_or_imprecise_dtypes=True))
+    gr0 = G(lambda: g.iota(T.ident[:], [[0, 8], [1, 16]], 0, 0, allow_small_or_imprecise_dtypes=True))
+    gr = V(lambda: v.tensor_scalar(T.ri[:], T.ident[:], -7.5, None, ADD), gr0)
+    gid = G(lambda: g.affine_select(T.tri[:], T.ones[:], [[1, 128]], EQ, 0.0, 0, -1), g0)
+    gn = G(lambda: g.iota(T.nrow[:], [[1, 16]], -16, 0, allow_small_or_imprecise_dtypes=True))
+    gc = G(lambda: g.iota(T.crow[:], [[16, 8]], 0, 0, allow_small_or_imprecise_dtypes=True))
+
+    s1 = S(lambda: sc.activation(T.trt[:, 1:512:4], T.trt[:, 0:512:4], COPY, scale=-1.0), g0)
+    srq = S(lambda: sc.activation(T.rqt[:, 0:512], T.zt[:], COPY), ztm)
+    srq2 = S(lambda: sc.activation(T.rqt[:, 512:576], T.zt[:, 0:64], COPY), ztm)
+    ez = [S((lambda b: lambda: sc.activation(T.et[:, 512 * b:512 * b + 512], T.zt[:], COPY))(b), ztm) for b in range(4)]
+    ed = [S((lambda b: lambda: sc.activation(T.et[:, 512 * b + b:512 * b + 512:4], T.tri[:], COPY))(b), gid, ez[b]) for b in range(4)]
+
+    pa = V(lambda: v.tensor_scalar(T.pj[:, 0:4], T.pi[:], 112, None, AND), gp)
+    pb = V(lambda: v.tensor_scalar(T.pj[:, 4:8], T.pi[:], 15, None, AND), gp)
+    pq = V(lambda: v.tensor_scalar(T.pj[:, 8:12], T.pi[:], 96, None, AND), gp)
+    pc = V(lambda: v.tensor_copy(T.pc[:, 0:12], T.pj[:, 0:12]), pa, pb, pq)
+    hi16, lo = T.pc[:, 0:1], T.pc[:, 4:5]
+    qoff = V(lambda: v.tensor_scalar(T.qoff[:], T.pc[:, 8:12], 4.0, None, MUL), pc)
+    qtr = quant("tr", "trt", 0, 128, 0, g0, s1, g2, g3)
+    b1m = V(lambda: v.memset(T.bt1[:], 0.0))
+    db1 = [D("y", "db1", T.bt1[32 * h:32 * h + 32, 512 * h:512 * h + 512], T.b1[32 * h:32 * h + 32, :], b1m) for h in range(4)]
+
+    qco = quant("co", "cot", 0, 128, 0, cot, dco)
+    qx = quant("x", "xt", 0, 128, 0, dx)
+    ms = mm(0, 128, "x", 0, "co", 0, True, True, qco, qx)
+    rmc = V(lambda: v.tensor_tensor_scan(T.rmc[:], T.neg[:, 0:8], T.p0[:, 0:8], LOW, MAX, MAX), ms, neg)
+    ge0 = V(lambda: v.tensor_scalar(T.mt[:, 0:32:4], T.rmc[:], T.rmc[:, 7:8], None, GE), rmc, mtm)
+    ge1 = V(lambda: v.tensor_scalar(T.mt[:, 5:32:4], T.rmc[:, 0:7], T.rmc[:, 7:8], None, GE), rmc, mtm)
+    qm = quant("m", "mt", 0, 128, 0, ge0, ge1, gm2, gm3)
+    mr = mm(1, 128, "tr", 0, "m", 0, True, True, qm, qtr)
+    val = V(lambda: v.tensor_reduce(T.val[:, 0:1], T.p1[:, 0:8], AxisListType.X, MAX), mr)
+    s16 = V(lambda: v.tensor_scalar(T.s16[:, 0:1], T.val[:, 0:1], R16, R16, ADD, SUB), val)
+    r0 = V(lambda: v.tensor_scalar(T.rqt[:, 0:512:4], T.ri[:], T.s16[:, 0:1], T.val[:, 0:1], ADD, EQ), s16, gr, srq)
+    r1 = V(lambda: v.tensor_scalar(T.rqt[:, 1:512:4], T.ri[:], T.s16[:, 0:1], T.val[:, 0:1], ADD, EQ), s16)
+    q0 = V(lambda: v.tensor_scalar(T.rqt[:, 512:576:4], T.qrow[:], T.s16[:, 0:1], hi16, EQ, MUL), gq, srq2, pc)
+    q1 = V(lambda: v.tensor_scalar(T.rqt[:, 513:576:4], T.qrow[:], T.s16[:, 0:1], lo, EQ, MUL), s16)
+    qrq = quant("rq", "rqt", 0, 144, 0, r0, r1, q0, q1)
+    ml = mm(6, 128, "rq", 0, "rq", 16, True, True, qrq)
+    loff = V(lambda: v.tensor_copy(T.loff[:], T.p6[:, 112:128]), ml)
+    sk, ss = pick("slot", 0, 256, "x", 128, "loff", 0, loff)
+    send(lambda d: K("slot", 32 * d, 32 * d + 32).bitcast(dt.uint8), K("land", 32 * me, 32 * me + 32).bitcast(dt.uint8), "ra" if me < 4 else "rb", False, sk)
+    send(lambda d: P("slot", 32 * d, 32 * d + 32), P("land", 32 * me, 32 * me + 32), "ra" if me < 4 else "rb", False, ss)
+    lk, ls = pick("land", 32 * me, 32 * me + 32, "x", 128, "loff", 2 * me, loff)
+
+    qb1 = quant("b1", "bt1", 0, 512, 0, *db1)
+    qe = quant("e", "et", 0, 512, 0, *ed)
+    en = S(lambda: sc.activation(T.en[:], T.et[:], COPY, scale=-1.0), *ed)
+    b2m = V(lambda: v.memset(T.bt2[:], 0.0))
+    db2 = [D("y", "db2", T.bt2[32 * h:32 * h + 32, 512 * h:512 * h + 512], T.b2[32 * h:32 * h + 32, :], b2m) for h in range(4)]
+    dw = D("y", "dw", T.wt[:], T.w[:])
+    mz = [V((lambda n: lambda: v.memset(T[n][:], 0.0))(n)) for n in ("m1", "m2")]
+    wrm = V(lambda: v.memset(T.wrow[:], -1.0))
+    qne = quant("ne", "en", 0, 512, 0, en)
+    ctm = V(lambda: v.memset(T.ct[:], 0.0))
+    htm = V(lambda: v.memset(T.ht[:], 0.0))
+    h1 = V(lambda: v.tensor_scalar(T.qone[:], T.qrow[:], T.s16[:, 0:1], None, EQ), s16)
+    l75 = V(lambda: v.tensor_scalar(T.lo75[:, 0:1], lo, -7.5, None, ADD), pc)
+    h5 = V(lambda: v.tensor_scalar(T.hr[:, 0:1], T.val[:, 0:1], T.s16[:, 0:1], 7.5, SUB, ADD), s16)
+    mk = V(lambda: v.tensor_scalar(T.mask8[:], T.crow[:], hi16, None, EQ), pc, gc)
+    h2 = V(lambda: v.tensor_tensor(T.qa[:], T.qone[:], T.nrow[:], MUL), h1, gn)
+    h4 = V(lambda: v.tensor_reduce(T.hk[:, 0:1], T.qone[:], AxisListType.X, ADD), h1)
+    c0 = V(lambda: v.tensor_scalar(T.ct[:, 0:512:4], T.ri[:], T.lo75[:, 0:1], 16.0, EQ, MUL), l75, ctm, gr)
+    c1 = V(lambda: v.tensor_scalar(T.ct[:, 1:512:4], T.ri[:], T.lo75[:, 0:1], None, EQ), l75)
+    h3 = V(lambda: v.tensor_reduce(T.ha[:, 0:1], T.qa[:], AxisListType.X, ADD), h2)
+    h6 = V(lambda: v.tensor_tensor(T.hrr[:, 0:1], T.hr[:, 0:1], T.hk[:, 0:1], MUL), h5, h4)
+    qc = quant("c", "ct", 0, 128, 0, c0, c1)
+    h7 = V(lambda: v.tensor_scalar(T.hb[:, 0:1], T.ha[:, 0:1], 16.0, None, ADD), h3)
+    h9 = V(lambda: v.tensor_scalar(T.ht[:, 1:32:4], T.mask8[:], T.hrr[:, 0:1], None, MUL), h6, mk, htm)
+    h8 = V(lambda: v.tensor_scalar(T.ht[:, 0:32:4], T.mask8[:], T.hb[:, 0:1], None, MUL), h7, mk, htm)
+    qh = quant("h", "ht", 0, 128, 0, h8, h9)
+    mh = mm(7, 128, "c", 0, "h", 0, True, True, qc, qh)
+    hoff = V(lambda: v.tensor_copy(T.hoff[:], T.p7[:, 0:8]), mh)
+    qz = [quant(n, "zt", 256, 384, 0, ztm) for n in ("hva", "hvb")]
+    qw = quant("w", "wt", 0, 128, 0, dw)
+    qb2 = quant("b2", "bt2", 0, 512, 0, *db2)
+
+    def level(lev, z, book, banks, zdeps, bdeps, between):
+        L = str(lev)
+        n, m, t, td, tt, off, rm, sg = ["%s%s" % (a, L) for a in ("n", "m", "t", "td", "tt", "off", "rm", "sg")]
+        mmx = [mm(banks[i], 512, z, 128 * i, book, 0, True, True, bdeps, *zdeps[i]) for i in (0, 1)]
+        between(mmx)
+        scan, sign = {}, {}
+        for i in (0, 1):
+            for h in range(4):
+                c = 512 * i + 128 * h
+                scan[i, h] = V((lambda i, h, c: lambda: v.tensor_tensor_scan(T[rm][:, c:c + 128], T.neg[:], T["p%d" % banks[i]][:, 128 * h:128 * h + 128], LOW, MAX, MAX))(i, h, c), mmx[i], neg)
+        for i in (0, 1):
+            for h in range(4):
+                c = 512 * i + 128 * h
+                sign[i, h] = S((lambda i, h, c: lambda: sc.activation(T[sg][:, c:c + 128], T[rm][:, c:c + 128], SIGN, bias=T[rm][:, c + 127:c + 128], scale=-1.0, accum_out=T[n][:, 2 * h + i:2 * h + i + 1]))(i, h, c), scan[i, h])
+        mv = []
+        for h in range(4):
+            for a in range(4):
+                o, w, dep = T[m][32 * h:32 * h + 32, a:8:4], T[n][32 * a:32 * a + 32, 2 * h:2 * h + 2], (sign[0, h], sign[1, h], mz[lev - 1])
+                if 4 * h + a < 10:
+                    mv.append(V((lambda o, w: lambda: v.tensor_copy(o, w))(o, w), *dep))
+                else:
+                    mv.append(S((lambda o, w: lambda: sc.activation(o, w, COPY))(o, w), *dep))
+        tr = V(lambda: v.transpose(T[t][:], T[m][:]), *mv)
+        dup = []
+        for a in (0, 1):
+            for u in (0, 1):
+                o, w = T[td][:, 32 * a + 16 * u:32 * a + 16 * u + 16], T[t][:, 16 * a:16 * a + 16]
+                if u == 0:
+                    dup.append(V((lambda o, w: lambda: v.tensor_copy(o, w))(o, w), tr))
+                else:
+                    dup.append(S((lambda o, w: lambda: sc.activation(o, w, COPY))(o, w), tr))
+        tr2 = V(lambda: v.transpose(T[tt][:], T[td][:]), *dup)
+        of = [V((lambda a: lambda: v.tensor_scalar(T[off][:, a:16:2], T[tt][:, 32 * a:32 * a + 8], T.qoff[:, 0:1], None, ADD))(a), tr2, qoff) for a in (0, 1)]
+        dn = [D("y", "dn" + L, T["ws" + L][:, 32 * h:32 * h + 32, 0], T[t][32 * h:32 * h + 8, 0:32], tr) for h in range(4)]
+        do = [D("y", "do" + L, T["wl" + L][me:me + 1, 32 * h:32 * h + 32, 0], T[t][32 * h + me:32 * h + me + 1, 0:32], tr) for h in range(4)]
+        return scan, of, dn, do
+
+    def flat(lev, do):
+        L = str(lev)
+        return [D("y", "df" + L, T.wrow[4 * lev - 4 + h:4 * lev - 3 + h, 0:256], T["wl" + L][:, 32 * h:32 * h + 32, 0], arrivals("rn" + L, range(8), 1, True), wrm, *do) for h in range(4)]
+
+    arr = [arrivals("ra", range(0, 4), 2, False), arrivals("rb", range(4, 8), 2, False)]
+    zd = [[arr[i]] + ([lk, ls] if me // 4 == i else []) for i in (0, 1)]
+    bank = {}
+
+    def unpack(mmx):
+        for b in range(4):
+            bank[0, b] = (2 + b, mm(2 + b, 128, "e", 128 * b, "land", 0, True, False, qe, *zd[0]))
+        for b in (0, 1):
+            bank[1, b] = (6 + b, mm(6 + b, 128, "e", 128 * b, "land", 128, True, False, qe, loff, hoff, *zd[1]))
+    scan1, of1, dn1, do1 = level(1, "land", "b1", (0, 1), zd, qb1, unpack)
+    for b in (2, 3):
+        bank[1, b] = (b - 2, mm(b - 2, 128, "e", 128 * b, "land", 128, True, False, *[scan1[b - 2, h] for h in range(4)]))
+    va = [pick("va", 128 * i, 128 * i + 128, "b1", 512, "off1", 8 * i, *of1) for i in (0, 1)]
+    send(lambda d: K("va", 32 * d, 32 * d + 32).bitcast(dt.uint8), K("hva", 32 * me, 32 * me + 32).bitcast(dt.uint8), "rva", False, va[0][0], va[1][0])
+    send(lambda d: P("va", 32 * d, 32 * d + 32), P("hva", 32 * me, 32 * me + 32), "rva", False, va[0][1], va[1][1])
+    send(lambda d: T.ws1[d], T.wl1[me], "rn1", True, *dn1)
+    qr, rc = [], {}
+    for i in (0, 1):
+        fin = [mm(bank[i, b][0], 128, "ne", 128 * b, "va", 128 * i, False, True, qne, *va[i]) for b in range(4)]
+        for b in range(4):
+            o, w = T.rt[:, 512 * i + b:512 * i + 512:4], T["p%d" % bank[i, b][0]][:, 0:128]
+            if b % 2 == 0:
+                rc[i, b] = V((lambda o, w: lambda: v.tensor_copy(o, w))(o, w), fin[b])
+            else:
+                rc[i, b] = S((lambda o, w: lambda: sc.activation(o, w, COPY))(o, w), fin[b])
+        qr.append(quant("r", "rt", 128 * i, 128 * i + 128, 512 * i, *[rc[i, b] for b in range(4)]))
+    ka, sa = pick("hva", 32 * me, 32 * me + 32, "b1", 512, "off1", 2 * me, *of1)
+
+    scan2, of2, dn2, do2 = level(2, "r", "b2", (2, 3), [[qr[0]], [qr[1]]], qb2, lambda mmx: None)
+    vb = [pick("vb", 128 * i, 128 * i + 128, "b2", 512, "off2", 8 * i, *of2) for i in (0, 1)]
+    send(lambda d: K("vb", 32 * d, 32 * d + 32).bitcast(dt.uint8), K("hvb", 32 * me, 32 * me + 32).bitcast(dt.uint8), "rvb", False, vb[0][0], vb[1][0])
+    send(lambda d: T.ws2[d], T.wl2[me], "rn2", True, *dn2)
+    send(lambda d: P("vb", 32 * d, 32 * d + 32), P("hvb", 32 * me, 32 * me + 32), "rvb", False, vb[0][1], vb[1][1])
+    kb, sb = pick("hvb", 32 * me, 32 * me + 32, "b2", 512, "off2", 2 * me, *of2)
+
+    oa = pick("oa", 0, 128, "hva", 384, "hoff", 0, hoff, qz[0], ka, sa, arrivals("rva", range(8), 2, False))
+    y1 = mm(4, 128, "w", 0, "oa", 0, True, False, qw, rc[0, 2], *oa)
+    D("y", "dst", T.oc[:, 0:512], K("oa", 0, 128).bitcast(dt.uint8), oa[0])
+    for k in range(4):
+        D("y", "dst", T.osc[4 * k:4 * k + 4, 0:128], T.s_oa[32 * k:32 * k + 4, :], oa[1])
+    f1 = flat(1, do1)
+    f2 = flat(2, do2)
+    ob = pick("ob", 0, 128, "hvb", 384, "hoff", 0, hoff, qz[1], kb, sb, arrivals("rvb", range(8), 2, False))
+    y2 = mm(4, 128, "w", 0, "ob", 0, False, True, *ob)
+    for k in range(4):
+        D("s", "dst", T.osc[4 * k:4 * k + 4, 128:256], T.s_ob[32 * k:32 * k + 4, :], ob[1])
+    D("y", "dst", T.oc[:, 512:1024], K("ob", 0, 128).bitcast(dt.uint8), ob[0])
+    yc = V(lambda: v.tensor_copy(T.yt[:], T.p4[:, 0:128]), y2)
+    D("y", "dst", T.y[:], T.yt[:], yc)
+    wn = V(lambda: v.tensor_copy(T.wnf[:], T.wrow[:].indirect(T.hoff[:])), hoff, *f1, *f2)
+    D("y", "dst", T.wn[:], T.wnf[0:8, :], wn)
+
+    total, at = {}, []
+    for q, fn, deps, sem, inc in ops:
+        if sem:
+            total[sem] = total.get(sem, 0) + inc
+        at.append((sem, total.get(sem, 0)))
+    total.update(expect)
+    known, most = {q: {} for q in queue}, {}
+
+    def wait(q, sem, n):
+        if known[q].get(sem, 0) < n:
+            queue[q].wait_ge(T.sem[sem], n)
+            known[q][sem] = n
+            most[sem] = max(most.get(sem, 0), n)
+    for q, fn, deps, sem, inc in ops:
+        need = {}
+        for d in deps:
+            s, n = d if isinstance(d, tuple) else at[d]
+            if s.startswith("d"):
+                n = total[s]
+            need[s] = max(need.get(s, 0), n)
+        for s in need:
+            wait(q, s, need[s])
+        ins = fn()
+        if sem:
+            ins.then_inc(T.sem[sem], inc)
+    for s in total:
+        if most.get(s, 0) < total[s]:
+            wait("g", s, total[s])

@@ -4,15 +4,15 @@ from concourse.mybir import dt, AluOpType, AxisListType, ActivationFunctionType
 BF, F32, I32, U16, COD, PL = "bfloat16", "float32", "int32", "uint16", "float8_e4m3fn_x4", "uint8"
 SCRATCH = {
     "xt": ("sbuf", [128, 512], BF), "cot": ("sbuf", [128, 512], BF), "wt": ("sbuf", [128, 512], BF),
-    "bt1": ("sbuf", [128, 2048], BF), "bt2": ("sbuf", [128, 2048], BF),
+    "br1": ("sbuf", [128, 512], BF), "br2": ("sbuf", [128, 512], BF), "bt1": ("sbuf", [128, 2048], BF), "bt2": ("sbuf", [128, 2048], BF),
     "et": ("sbuf", [128, 2048], BF), "en": ("sbuf", [128, 2048], BF),
     "trt": ("sbuf", [128, 512], BF), "ct": ("sbuf", [128, 512], BF), "mt": ("sbuf", [128, 512], BF),
     "rqt": ("sbuf", [128, 576], BF), "ht": ("sbuf", [128, 512], BF), "zt": ("sbuf", [128, 512], BF),
     "rt": ("sbuf", [128, 1024], BF),
     "ones": ("sbuf", [128, 128], BF), "ident": ("sbuf", [128, 128], BF), "tri": ("sbuf", [128, 128], BF),
     "neg": ("sbuf", [128, 128], F32), "c75": ("sbuf", [128, 8], BF), "c128": ("sbuf", [128, 8], BF),
-    "ri": ("sbuf", [128, 128], BF), "qrow": ("sbuf", [128, 16], F32), "nrow": ("sbuf", [128, 16], F32),
-    "crow": ("sbuf", [128, 8], F32), "pi": ("sbuf", [128, 4], I32), "pj": ("sbuf", [128, 16], I32),
+    "rj": ("sbuf", [128, 128], BF), "ri": ("sbuf", [128, 128], BF), "qrow": ("sbuf", [128, 16], F32), "nrow": ("sbuf", [128, 16], F32),
+    "crow": ("sbuf", [128, 8], F32), "pi": ("sbuf", [128, 4], I32), "pj": ("sbuf", [128, 16], I32), "qm4": ("sbuf", [128, 4], F32),
     "pc": ("sbuf", [128, 16], F32), "lo75": ("sbuf", [128, 4], F32), "qoff": ("sbuf", [128, 4], F32), "mask8": ("sbuf", [128, 8], F32),
     "rmc": ("sbuf", [128, 8], F32), "val": ("sbuf", [128, 4], F32), "s16": ("sbuf", [128, 4], F32),
     "qone": ("sbuf", [128, 16], F32), "qa": ("sbuf", [128, 16], F32), "ha": ("sbuf", [128, 4], F32), "hb": ("sbuf", [128, 4], F32),
@@ -32,7 +32,7 @@ for _n, _w in (("x", 128), ("co", 128), ("w", 128), ("b1", 512), ("b2", 512), ("
     SCRATCH["s_" + _n] = ("sbuf", [128, _w], PL)
 for _n in range(8):
     SCRATCH["p%d" % _n] = ("psum", [128, 512], F32)
-SEMAPHORES = ["cv", "cs", "ce", "cg", "dx", "dco", "db1", "db2", "dw", "dn1", "dn2", "do1", "do2", "df1", "df2", "dst",
+SEMAPHORES = ["cv", "cs", "ce", "cg", "dx", "dco", "db1", "db2", "dw", "dn1", "dn2", "do1", "do2", "df1", "df2", "dst", "dso",
               "ra", "rb", "rva", "rvb", "rn1", "rn2", "loc"]
 
 ADD, SUB, MUL, MAX = AluOpType.add, AluOpType.subtract, AluOpType.mult, AluOpType.max
@@ -63,6 +63,14 @@ def rank_program(g, core, T, topo):
     v, sc, te = g.vector, g.scalar, g.tensor
     K = lambda n, a, b: T["k_" + n][:, a:b]
     P = lambda n, a, b: T["s_" + n][:, a:b]
+
+    def ts(out, in0, s1, s2, op0, op1, *deps):
+        return V(lambda: v.tensor_scalar(out, in0, s1, s2, op0) if op1 is None else v.tensor_scalar(out, in0, s1, s2, op0, op1), *deps)
+
+    def act(out, in_, *deps):
+        return S(lambda: sc.activation(out, in_, COPY), *deps)
+
+    def fill(ap, c): return V(lambda: v.memset(ap, c))
 
     def quant(n, tile, a, b, src, *deps):
         return V(lambda: v.quantize_mx(K(n, a, b), P(n, a, b), T[tile][:, src:src + 4 * (b - a)]), *deps)
@@ -95,72 +103,69 @@ def rank_program(g, core, T, topo):
                 tr.append(RemoteDMATransfer(dst_ids=[DstId(rid=rid, pnc=pid)], dma_engine_mask=m, remote_sem=T.sem[sem], src=src(d), dst=dst))
             return g.remote_dma_fused(tr, local_sem=T.sem["loc"])
         for d in others:
-            n = 1 if one else len(eng[d])
-            expect["loc"] = expect.get("loc", 0) + n
+            expect["loc"] = expect.get("loc", 0) + (1 if one else len(eng[d]))
         return add("g", call, deps, "")
 
-    def per(s, one):
-        c = T.cores[s]
-        return 1 if one else len(topo.engines(c, core)) // 8
-
     def arrivals(sem, ranks, n, one):
-        expect[sem] = n * sum(per(s, one) for s in ranks if s != me)
+        expect[sem] = n * sum(1 if one else len(topo.engines(T.cores[s], core)) // 8 for s in ranks if s != me)
         return (sem, expect[sem])
 
-    dx = D("y", "dx", T.xt[:], T.x[:])
     dco = D("s", "dco", T.cot[:, 0:32], T.co[:, 0:32])
-    ones = V(lambda: v.memset(T.ones[:], 1.0))
-    ztm = V(lambda: v.memset(T.zt[:], 0.0))
-    mtm = V(lambda: v.memset(T.mt[:], 0.0))
-    c75 = V(lambda: v.memset(T.c75[:], -7.5))
-    cot = V(lambda: v.memset(T.cot[:, 32:512], 0.0))
-    neg = V(lambda: v.memset(T.neg[:], LOW))
+    dx = D("y", "dx", T.xt[:], T.x[:])
+    db1 = D("y", "db1", T.br1[:], T.b1[:])
+    db2 = D("y", "db2", T.br2[:], T.b2[:])
+    dw = D("y", "dw", T.wt[:], T.w[:])
 
-    ga = G(lambda: g.affine_select(T.tri[:], T.ones[:], [[1, 128]], GE, 0.0, 0, -1), ones)
-    g0 = G(lambda: g.affine_select(T.trt[:, 0:512:4], T.tri[:], [[1, 128]], NE, 1024.0, 0, -1), ga)
-    g2 = G(lambda: g.affine_select(T.trt[:, 2:512:4], T.ones[:], [[0, 128]], EQ, 0.0, 0, 1), ones)
-    g3 = G(lambda: g.affine_select(T.trt[:, 3:512:4], T.ones[:], [[0, 128]], EQ, 0.0, -1, 1), ones)
-    gi = G(lambda: g.iota(T.c128[:], [[128, 8]], 0, 0, allow_small_or_imprecise_dtypes=True))
-    gm2 = G(lambda: g.affine_select(T.mt[:, 2:32:4], T.c128[:], [[0, 8]], EQ, 0.0, 0, 1), gi, mtm)
-    gm3 = G(lambda: g.affine_select(T.mt[:, 3:32:4], T.c75[:], [[0, 8]], EQ, 0.0, -1, 1), c75, mtm)
+    ones = fill(T.ones[:], 1.0)
+    cot = fill(T.cot[:, 32:512], 0.0)
+    ztm = fill(T.zt[:], 0.0)
+    mtm = fill(T.mt[:], 0.0)
+    c75 = fill(T.c75[:], -7.5)
+    neg = fill(T.neg[:], LOW)
+
+    def affine(out, in_, step, n, op, f, base, cm, *deps): return G(lambda: g.affine_select(out, in_, [[step, n]], op, f, base, cm), *deps)
+    def iota(out, pattern, base, cm): return G(lambda: g.iota(out, pattern, base, cm, allow_small_or_imprecise_dtypes=True))
+    ga = affine(T.tri[:], T.ones[:], 1, 128, GE, 0.0, 0, -1, ones)
+    g2 = affine(T.trt[:, 2:512:4], T.ones[:], 0, 128, EQ, 0.0, 0, 1, ones)
+    g0 = affine(T.trt[:, 0:512:4], T.tri[:], 1, 128, NE, 1024.0, 0, -1, ga)
+    g3 = affine(T.trt[:, 3:512:4], T.ones[:], 0, 128, EQ, 0.0, -1, 1, ones)
+    gi = iota(T.c128[:], [[128, 8]], 0, 0)
     gp = G(lambda: g.iota(T.pi[:], [[0, 4]], 0, 1))
-    gq = G(lambda: g.iota(T.qrow[:], [[128, 8], [16, 2]], 1024, 0, allow_small_or_imprecise_dtypes=True))
-    gr0 = G(lambda: g.iota(T.ident[:], [[0, 8], [1, 16]], 0, 0, allow_small_or_imprecise_dtypes=True))
-    gr = V(lambda: v.tensor_scalar(T.ri[:], T.ident[:], -7.5, None, ADD), gr0)
-    gid = G(lambda: g.affine_select(T.tri[:], T.ones[:], [[1, 128]], EQ, 0.0, 0, -1), g0)
-    gn = G(lambda: g.iota(T.nrow[:], [[1, 16]], -16, 0, allow_small_or_imprecise_dtypes=True))
-    gc = G(lambda: g.iota(T.crow[:], [[16, 8]], 0, 0, allow_small_or_imprecise_dtypes=True))
+    gm2 = affine(T.mt[:, 2:32:4], T.c128[:], 0, 8, EQ, 0.0, 0, 1, gi, mtm)
+    gm3 = affine(T.mt[:, 3:32:4], T.c75[:], 0, 8, EQ, 0.0, -1, 1, c75, mtm)
+    gr0 = iota(T.rj[:], [[0, 8], [1, 16]], 0, 0)
+    gq = iota(T.qrow[:], [[128, 8], [16, 2]], 1024, 0)
+    gid = affine(T.ident[:], T.ones[:], 1, 128, EQ, 0.0, 0, -1, ones)
+    gn = iota(T.nrow[:], [[1, 16]], -16, 0)
+    gc = iota(T.crow[:], [[16, 8]], 0, 0)
 
+    srq = act(T.rqt[:, 0:512], T.zt[:], ztm)
+    srq2 = act(T.rqt[:, 512:576], T.zt[:, 0:64], ztm)
     s1 = S(lambda: sc.activation(T.trt[:, 1:512:4], T.trt[:, 0:512:4], COPY, scale=-1.0), g0)
-    srq = S(lambda: sc.activation(T.rqt[:, 0:512], T.zt[:], COPY), ztm)
-    srq2 = S(lambda: sc.activation(T.rqt[:, 512:576], T.zt[:, 0:64], COPY), ztm)
-    ez = [S((lambda b: lambda: sc.activation(T.et[:, 512 * b:512 * b + 512], T.zt[:], COPY))(b), ztm) for b in range(4)]
-    ed = [S((lambda b: lambda: sc.activation(T.et[:, 512 * b + b:512 * b + 512:4], T.tri[:], COPY))(b), gid, ez[b]) for b in range(4)]
-
-    pa = V(lambda: v.tensor_scalar(T.pj[:, 0:4], T.pi[:], 112, None, AND), gp)
-    pb = V(lambda: v.tensor_scalar(T.pj[:, 4:8], T.pi[:], 15, None, AND), gp)
-    pq = V(lambda: v.tensor_scalar(T.pj[:, 8:12], T.pi[:], 96, None, AND), gp)
-    pc = V(lambda: v.tensor_copy(T.pc[:, 0:12], T.pj[:, 0:12]), pa, pb, pq)
-    hi16, lo = T.pc[:, 0:1], T.pc[:, 4:5]
-    qoff = V(lambda: v.tensor_scalar(T.qoff[:], T.pc[:, 8:12], 4.0, None, MUL), pc)
-    qtr = quant("tr", "trt", 0, 128, 0, g0, s1, g2, g3)
-    b1m = V(lambda: v.memset(T.bt1[:], 0.0))
-    db1 = [D("y", "db1", T.bt1[32 * h:32 * h + 32, 512 * h:512 * h + 512], T.b1[32 * h:32 * h + 32, :], b1m) for h in range(4)]
+    gr = S(lambda: sc.activation(T.ri[:], T.rj[:], COPY, bias=-7.5), gr0)
+    ez = [act(T.et[:, 512 * b:512 * b + 512], T.zt[:], ztm) for b in range(4)]
+    ed = [act(T.et[:, 512 * b + b:512 * b + 512:4], T.ident[:], gid, ez[b]) for b in range(4)]
 
     qco = quant("co", "cot", 0, 128, 0, cot, dco)
     qx = quant("x", "xt", 0, 128, 0, dx)
     ms = mm(0, 128, "x", 0, "co", 0, True, True, qco, qx)
+    qtr = quant("tr", "trt", 0, 128, 0, g0, s1, g2, g3)
     rmc = V(lambda: v.tensor_tensor_scan(T.rmc[:], T.neg[:, 0:8], T.p0[:, 0:8], LOW, MAX, MAX), ms, neg)
-    ge0 = V(lambda: v.tensor_scalar(T.mt[:, 0:32:4], T.rmc[:], T.rmc[:, 7:8], None, GE), rmc, mtm)
-    ge1 = V(lambda: v.tensor_scalar(T.mt[:, 5:32:4], T.rmc[:, 0:7], T.rmc[:, 7:8], None, GE), rmc, mtm)
+    ge0 = ts(T.mt[:, 0:32:4], T.rmc[:], T.rmc[:, 7:8], None, GE, None, rmc, mtm)
+    ge1 = ts(T.mt[:, 5:32:4], T.rmc[:, 0:7], T.rmc[:, 7:8], None, GE, None, rmc, mtm)
     qm = quant("m", "mt", 0, 128, 0, ge0, ge1, gm2, gm3)
     mr = mm(1, 128, "tr", 0, "m", 0, True, True, qm, qtr)
-    val = V(lambda: v.tensor_reduce(T.val[:, 0:1], T.p1[:, 0:8], AxisListType.X, MAX), mr)
-    s16 = V(lambda: v.tensor_scalar(T.s16[:, 0:1], T.val[:, 0:1], R16, R16, ADD, SUB), val)
-    r0 = V(lambda: v.tensor_scalar(T.rqt[:, 0:512:4], T.ri[:], T.s16[:, 0:1], T.val[:, 0:1], ADD, EQ), s16, gr, srq)
-    r1 = V(lambda: v.tensor_scalar(T.rqt[:, 1:512:4], T.ri[:], T.s16[:, 0:1], T.val[:, 0:1], ADD, EQ), s16)
-    q0 = V(lambda: v.tensor_scalar(T.rqt[:, 512:576:4], T.qrow[:], T.s16[:, 0:1], hi16, EQ, MUL), gq, srq2, pc)
-    q1 = V(lambda: v.tensor_scalar(T.rqt[:, 513:576:4], T.qrow[:], T.s16[:, 0:1], lo, EQ, MUL), s16)
+    pa = ts(T.pj[:, 0:4], T.pi[:], 112, None, AND, None, gp)
+    pb = ts(T.pj[:, 4:8], T.pi[:], 15, None, AND, None, gp)
+    pq = ts(T.pj[:, 8:12], T.pi[:], 96, None, AND, None, gp)
+    pc = V(lambda: v.tensor_copy(T.pc[:, 0:12], T.pj[:, 0:12]), pa, pb, pq)
+    hi16, lo, val16, s16a = T.pc[:, 0:1], T.pc[:, 4:5], T.val[:, 0:1], T.s16[:, 0:1]
+    val = V(lambda: v.tensor_reduce(val16, T.p1[:, 0:8], AxisListType.X, MAX), mr)
+    s16 = ts(s16a, val16, R16, R16, ADD, SUB, val)
+    r0 = ts(T.rqt[:, 0:512:4], T.ri[:], s16a, val16, ADD, EQ, s16, gr, srq)
+    r1 = ts(T.rqt[:, 1:512:4], T.ri[:], s16a, val16, ADD, EQ, s16)
+    q0 = ts(T.rqt[:, 512:576:4], T.qrow[:], s16a, hi16, EQ, MUL, gq, srq2, pc)
+    q1 = ts(T.rqt[:, 513:576:4], T.qrow[:], s16a, lo, EQ, MUL, s16)
     qrq = quant("rq", "rqt", 0, 144, 0, r0, r1, q0, q1)
     ml = mm(6, 128, "rq", 0, "rq", 16, True, True, qrq)
     loff = V(lambda: v.tensor_copy(T.loff[:], T.p6[:, 112:128]), ml)
@@ -169,37 +174,26 @@ def rank_program(g, core, T, topo):
     send(lambda d: P("slot", 32 * d, 32 * d + 32), P("land", 32 * me, 32 * me + 32), "ra" if me < 4 else "rb", False, ss)
     lk, ls = pick("land", 32 * me, 32 * me + 32, "x", 128, "loff", 2 * me, loff)
 
-    qb1 = quant("b1", "bt1", 0, 512, 0, *db1)
+    qsel = [ts(T.qm4[:, h:h + 1], T.pc[:, 8:9], 32.0 * h, None, EQ, None, pc) for h in range(4)]
+    qoff = ts(T.qoff[:], T.pc[:, 8:12], 4.0, None, MUL, None, pc)
+
+    def books(i, load):
+        o = []
+        for h in range(4):
+            t, r, m = T["bt%d" % i][:, 512 * h:512 * h + 512], T["br%d" % i][:], T.qm4[:, h:h + 1]
+            if h < 2:
+                o.append(ts(t, r, m, None, MUL, None, qsel[h], load))
+            else:
+                o.append(S((lambda t, r, m: lambda: sc.activation(t, r, COPY, scale=m))(t, r, m), qsel[h], load))
+        return o
+    bk1 = books(1, db1)
     qe = quant("e", "et", 0, 512, 0, *ed)
+    qb1 = quant("b1", "bt1", 0, 512, 0, *bk1)
     en = S(lambda: sc.activation(T.en[:], T.et[:], COPY, scale=-1.0), *ed)
-    b2m = V(lambda: v.memset(T.bt2[:], 0.0))
-    db2 = [D("y", "db2", T.bt2[32 * h:32 * h + 32, 512 * h:512 * h + 512], T.b2[32 * h:32 * h + 32, :], b2m) for h in range(4)]
-    dw = D("y", "dw", T.wt[:], T.w[:])
-    mz = [V((lambda n: lambda: v.memset(T[n][:], 0.0))(n)) for n in ("m1", "m2")]
-    wrm = V(lambda: v.memset(T.wrow[:], -1.0))
+    mz = [fill(T[n][:], 0.0) for n in ("m1", "m2")]
+    bk2 = books(2, db2)
     qne = quant("ne", "en", 0, 512, 0, en)
-    ctm = V(lambda: v.memset(T.ct[:], 0.0))
-    htm = V(lambda: v.memset(T.ht[:], 0.0))
-    h1 = V(lambda: v.tensor_scalar(T.qone[:], T.qrow[:], T.s16[:, 0:1], None, EQ), s16)
-    l75 = V(lambda: v.tensor_scalar(T.lo75[:, 0:1], lo, -7.5, None, ADD), pc)
-    h5 = V(lambda: v.tensor_scalar(T.hr[:, 0:1], T.val[:, 0:1], T.s16[:, 0:1], 7.5, SUB, ADD), s16)
-    mk = V(lambda: v.tensor_scalar(T.mask8[:], T.crow[:], hi16, None, EQ), pc, gc)
-    h2 = V(lambda: v.tensor_tensor(T.qa[:], T.qone[:], T.nrow[:], MUL), h1, gn)
-    h4 = V(lambda: v.tensor_reduce(T.hk[:, 0:1], T.qone[:], AxisListType.X, ADD), h1)
-    c0 = V(lambda: v.tensor_scalar(T.ct[:, 0:512:4], T.ri[:], T.lo75[:, 0:1], 16.0, EQ, MUL), l75, ctm, gr)
-    c1 = V(lambda: v.tensor_scalar(T.ct[:, 1:512:4], T.ri[:], T.lo75[:, 0:1], None, EQ), l75)
-    h3 = V(lambda: v.tensor_reduce(T.ha[:, 0:1], T.qa[:], AxisListType.X, ADD), h2)
-    h6 = V(lambda: v.tensor_tensor(T.hrr[:, 0:1], T.hr[:, 0:1], T.hk[:, 0:1], MUL), h5, h4)
-    qc = quant("c", "ct", 0, 128, 0, c0, c1)
-    h7 = V(lambda: v.tensor_scalar(T.hb[:, 0:1], T.ha[:, 0:1], 16.0, None, ADD), h3)
-    h9 = V(lambda: v.tensor_scalar(T.ht[:, 1:32:4], T.mask8[:], T.hrr[:, 0:1], None, MUL), h6, mk, htm)
-    h8 = V(lambda: v.tensor_scalar(T.ht[:, 0:32:4], T.mask8[:], T.hb[:, 0:1], None, MUL), h7, mk, htm)
-    qh = quant("h", "ht", 0, 128, 0, h8, h9)
-    mh = mm(7, 128, "c", 0, "h", 0, True, True, qc, qh)
-    hoff = V(lambda: v.tensor_copy(T.hoff[:], T.p7[:, 0:8]), mh)
-    qz = [quant(n, "zt", 256, 384, 0, ztm) for n in ("hva", "hvb")]
-    qw = quant("w", "wt", 0, 128, 0, dw)
-    qb2 = quant("b2", "bt2", 0, 512, 0, *db2)
+    qb2 = quant("b2", "bt2", 0, 512, 0, *bk2)
 
     def level(lev, z, book, banks, zdeps, bdeps, between):
         L = str(lev)
@@ -222,7 +216,7 @@ def rank_program(g, core, T, topo):
                 if 4 * h + a < 10:
                     mv.append(V((lambda o, w: lambda: v.tensor_copy(o, w))(o, w), *dep))
                 else:
-                    mv.append(S((lambda o, w: lambda: sc.activation(o, w, COPY))(o, w), *dep))
+                    mv.append(act(o, w, *dep))
         tr = V(lambda: v.transpose(T[t][:], T[m][:]), *mv)
         dup = []
         for a in (0, 1):
@@ -231,16 +225,12 @@ def rank_program(g, core, T, topo):
                 if u == 0:
                     dup.append(V((lambda o, w: lambda: v.tensor_copy(o, w))(o, w), tr))
                 else:
-                    dup.append(S((lambda o, w: lambda: sc.activation(o, w, COPY))(o, w), tr))
+                    dup.append(act(o, w, tr))
         tr2 = V(lambda: v.transpose(T[tt][:], T[td][:]), *dup)
-        of = [V((lambda a: lambda: v.tensor_scalar(T[off][:, a:16:2], T[tt][:, 32 * a:32 * a + 8], T.qoff[:, 0:1], None, ADD))(a), tr2, qoff) for a in (0, 1)]
+        of = [ts(T[off][:, a:16:2], T[tt][:, 32 * a:32 * a + 8], T.qoff[:, 0:1], None, ADD, None, tr2, qoff) for a in (0, 1)]
         dn = [D("y", "dn" + L, T["ws" + L][:, 32 * h:32 * h + 32, 0], T[t][32 * h:32 * h + 8, 0:32], tr) for h in range(4)]
         do = [D("y", "do" + L, T["wl" + L][me:me + 1, 32 * h:32 * h + 32, 0], T[t][32 * h + me:32 * h + me + 1, 0:32], tr) for h in range(4)]
         return scan, of, dn, do
-
-    def flat(lev, do):
-        L = str(lev)
-        return [D("y", "df" + L, T.wrow[4 * lev - 4 + h:4 * lev - 3 + h, 0:256], T["wl" + L][:, 32 * h:32 * h + 32, 0], arrivals("rn" + L, range(8), 1, True), wrm, *do) for h in range(4)]
 
     arr = [arrivals("ra", range(0, 4), 2, False), arrivals("rb", range(4, 8), 2, False)]
     zd = [[arr[i]] + ([lk, ls] if me // 4 == i else []) for i in (0, 1)]
@@ -250,7 +240,7 @@ def rank_program(g, core, T, topo):
         for b in range(4):
             bank[0, b] = (2 + b, mm(2 + b, 128, "e", 128 * b, "land", 0, True, False, qe, *zd[0]))
         for b in (0, 1):
-            bank[1, b] = (6 + b, mm(6 + b, 128, "e", 128 * b, "land", 128, True, False, qe, loff, hoff, *zd[1]))
+            bank[1, b] = (6 + b, mm(6 + b, 128, "e", 128 * b, "land", 128, True, False, qe, loff, *zd[1]))
     scan1, of1, dn1, do1 = level(1, "land", "b1", (0, 1), zd, qb1, unpack)
     for b in (2, 3):
         bank[1, b] = (b - 2, mm(b - 2, 128, "e", 128 * b, "land", 128, True, False, *[scan1[b - 2, h] for h in range(4)]))
@@ -266,16 +256,44 @@ def rank_program(g, core, T, topo):
             if b % 2 == 0:
                 rc[i, b] = V((lambda o, w: lambda: v.tensor_copy(o, w))(o, w), fin[b])
             else:
-                rc[i, b] = S((lambda o, w: lambda: sc.activation(o, w, COPY))(o, w), fin[b])
+                rc[i, b] = act(o, w, fin[b])
         qr.append(quant("r", "rt", 128 * i, 128 * i + 128, 512 * i, *[rc[i, b] for b in range(4)]))
-    ka, sa = pick("hva", 32 * me, 32 * me + 32, "b1", 512, "off1", 2 * me, *of1)
 
     scan2, of2, dn2, do2 = level(2, "r", "b2", (2, 3), [[qr[0]], [qr[1]]], qb2, lambda mmx: None)
     vb = [pick("vb", 128 * i, 128 * i + 128, "b2", 512, "off2", 8 * i, *of2) for i in (0, 1)]
     send(lambda d: K("vb", 32 * d, 32 * d + 32).bitcast(dt.uint8), K("hvb", 32 * me, 32 * me + 32).bitcast(dt.uint8), "rvb", False, vb[0][0], vb[1][0])
     send(lambda d: T.ws2[d], T.wl2[me], "rn2", True, *dn2)
     send(lambda d: P("vb", 32 * d, 32 * d + 32), P("hvb", 32 * me, 32 * me + 32), "rvb", False, vb[0][1], vb[1][1])
+
+    ka, sa = pick("hva", 32 * me, 32 * me + 32, "b1", 512, "off1", 2 * me, *of1)
     kb, sb = pick("hvb", 32 * me, 32 * me + 32, "b2", 512, "off2", 2 * me, *of2)
+    ha, hb, hk, hr, hrr = T.ha[:, 0:1], T.hb[:, 0:1], T.hk[:, 0:1], T.hr[:, 0:1], T.hrr[:, 0:1]
+    h1 = ts(T.qone[:], T.qrow[:], s16a, None, EQ, None, s16)
+    l75 = ts(T.lo75[:, 0:1], lo, -7.5, None, ADD, None, pc)
+    ctm = fill(T.ct[:], 0.0)
+    htm = fill(T.ht[:], 0.0)
+    h5 = ts(hr, val16, s16a, 7.5, SUB, ADD, s16)
+    mk = ts(T.mask8[:], T.crow[:], hi16, None, EQ, None, pc, gc)
+    h2 = V(lambda: v.tensor_tensor(T.qa[:], T.qone[:], T.nrow[:], MUL), h1, gn)
+    h4 = V(lambda: v.tensor_reduce(hk, T.qone[:], AxisListType.X, ADD), h1)
+    c0 = ts(T.ct[:, 0:512:4], T.ri[:], T.lo75[:, 0:1], 16.0, EQ, MUL, l75, ctm, gr)
+    c1 = ts(T.ct[:, 1:512:4], T.ri[:], T.lo75[:, 0:1], None, EQ, None, l75)
+    h3 = V(lambda: v.tensor_reduce(ha, T.qa[:], AxisListType.X, ADD), h2)
+    h6 = V(lambda: v.tensor_tensor(hrr, hr, hk, MUL), h5, h4)
+    qc = quant("c", "ct", 0, 128, 0, c0, c1)
+    h7 = ts(hb, ha, 16.0, None, ADD, None, h3)
+    h9 = ts(T.ht[:, 1:32:4], T.mask8[:], hrr, None, MUL, None, h6, mk, htm)
+    h8 = ts(T.ht[:, 0:32:4], T.mask8[:], hb, None, MUL, None, h7, mk, htm)
+    qh = quant("h", "ht", 0, 128, 0, h8, h9)
+    mh = mm(5, 128, "c", 0, "h", 0, True, True, qc, qh, rc[0, 3])
+    wrm = fill(T.wrow[:], -1.0)
+    qz = [quant(n, "zt", 256, 384, 0, ztm) for n in ("hva", "hvb")]
+    qw = quant("w", "wt", 0, 128, 0, dw)
+    hoff = V(lambda: v.tensor_copy(T.hoff[:], T.p5[:, 0:8]), mh)
+
+    def flat(lev, do):
+        L = str(lev)
+        return [D("y", "df" + L, T.wrow[4 * lev - 4 + h:4 * lev - 3 + h, 0:256], T["wl" + L][:, 32 * h:32 * h + 32, 0], arrivals("rn" + L, range(8), 1, True), wrm, *do) for h in range(4)]
 
     oa = pick("oa", 0, 128, "hva", 384, "hoff", 0, hoff, qz[0], ka, sa, arrivals("rva", range(8), 2, False))
     y1 = mm(4, 128, "w", 0, "oa", 0, True, False, qw, rc[0, 2], *oa)
@@ -286,11 +304,11 @@ def rank_program(g, core, T, topo):
     f2 = flat(2, do2)
     ob = pick("ob", 0, 128, "hvb", 384, "hoff", 0, hoff, qz[1], kb, sb, arrivals("rvb", range(8), 2, False))
     y2 = mm(4, 128, "w", 0, "ob", 0, False, True, *ob)
+    D("s", "dso", T.oc[:, 512:1024], K("ob", 0, 128).bitcast(dt.uint8), ob[0])
     for k in range(4):
-        D("s", "dst", T.osc[4 * k:4 * k + 4, 128:256], T.s_ob[32 * k:32 * k + 4, :], ob[1])
-    D("y", "dst", T.oc[:, 512:1024], K("ob", 0, 128).bitcast(dt.uint8), ob[0])
+        D("s", "dso", T.osc[4 * k:4 * k + 4, 128:256], T.s_ob[32 * k:32 * k + 4, :], ob[1])
     yc = V(lambda: v.tensor_copy(T.yt[:], T.p4[:, 0:128]), y2)
-    D("y", "dst", T.y[:], T.yt[:], yc)
+    D("s", "dso", T.y[:], T.yt[:], yc)
     wn = V(lambda: v.tensor_copy(T.wnf[:], T.wrow[:].indirect(T.hoff[:])), hoff, *f1, *f2)
     D("y", "dst", T.wn[:], T.wnf[0:8, :], wn)
 

@@ -22,7 +22,7 @@ SCRATCH = {
     "n1": ("sbuf", [128, 8], F32), "n2": ("sbuf", [128, 8], F32), "m1": ("sbuf", [128, 32], BF), "m2": ("sbuf", [128, 32], BF),
     "t1": ("sbuf", [128, 32], BF), "t2": ("sbuf", [128, 32], BF), "td1": ("sbuf", [128, 64], BF), "td2": ("sbuf", [128, 64], BF),
     "tt1": ("sbuf", [128, 64], BF), "tt2": ("sbuf", [128, 64], BF), "off1": ("sbuf", [128, 16], U16), "off2": ("sbuf", [128, 16], U16),
-    "ws1": ("dram", [8, 128, 1], BF), "ws2": ("dram", [8, 128, 1], BF), "wl1": ("dram", [8, 128, 1], BF), "wl2": ("dram", [8, 128, 1], BF),
+    "ws1": ("dram", [8, 128, 1], BF), "wl1": ("dram", [8, 128, 1], BF), "wl2": ("dram", [8, 128, 1], BF),
     "wrow": ("sbuf", [128, 272], BF), "wnf": ("sbuf", [128, 128], F32), "yt": ("sbuf", [128, 128], F32),
 }
 for _n, _w in (("x", 128), ("co", 128), ("w", 128), ("b1", 512), ("b2", 512), ("e", 512), ("ne", 512), ("tr", 128), ("c", 128),
@@ -32,7 +32,7 @@ for _n, _w in (("x", 128), ("co", 128), ("w", 128), ("b1", 512), ("b2", 512), ("
     SCRATCH["s_" + _n] = ("sbuf", [128, _w], PL)
 for _n in range(8):
     SCRATCH["p%d" % _n] = ("psum", [128, 512], F32)
-SEMAPHORES = ["cv", "cs", "ce", "cg", "dx", "dco", "db1", "db2", "dw", "dn1", "dn2", "do1", "do2", "df1", "df2", "dst", "dso",
+SEMAPHORES = ["cv", "cs", "ce", "cg", "dx", "dco", "db1", "db2", "dw", "dn1", "do1", "do2", "df1", "df2", "dst", "dso",
               "ra", "rb", "rva", "rvb", "rn1", "rn2", "loc"]
 
 ADD, SUB, MUL, MAX = AluOpType.add, AluOpType.subtract, AluOpType.mult, AluOpType.max
@@ -67,8 +67,9 @@ def rank_program(g, core, T, topo):
     def ts(out, in0, s1, s2, op0, op1, *deps):
         return V(lambda: v.tensor_scalar(out, in0, s1, s2, op0) if op1 is None else v.tensor_scalar(out, in0, s1, s2, op0, op1), *deps)
 
-    def act(out, in_, *deps):
-        return S(lambda: sc.activation(out, in_, COPY), *deps)
+    def cp(out, in_, *deps): return V(lambda: v.tensor_copy(out, in_), *deps)
+
+    def act(out, in_, *deps): return S(lambda: sc.activation(out, in_, COPY), *deps)
 
     def fill(ap, c): return V(lambda: v.memset(ap, c))
 
@@ -122,6 +123,7 @@ def rank_program(g, core, T, topo):
     mtm = fill(T.mt[:], 0.0)
     c75 = fill(T.c75[:], -7.5)
     neg = fill(T.neg[:], LOW)
+    enm = fill(T.en[:], 0.0)
 
     def affine(out, in_, step, n, op, f, base, cm, *deps): return G(lambda: g.affine_select(out, in_, [[step, n]], op, f, base, cm), *deps)
     def iota(out, pattern, base, cm): return G(lambda: g.iota(out, pattern, base, cm, allow_small_or_imprecise_dtypes=True))
@@ -158,7 +160,7 @@ def rank_program(g, core, T, topo):
     pa = ts(T.pj[:, 0:4], T.pi[:], 112, None, AND, None, gp)
     pb = ts(T.pj[:, 4:8], T.pi[:], 15, None, AND, None, gp)
     pq = ts(T.pj[:, 8:12], T.pi[:], 96, None, AND, None, gp)
-    pc = V(lambda: v.tensor_copy(T.pc[:, 0:12], T.pj[:, 0:12]), pa, pb, pq)
+    pc = cp(T.pc[:, 0:12], T.pj[:, 0:12], pa, pb, pq)
     hi16, lo, val16, s16a = T.pc[:, 0:1], T.pc[:, 4:5], T.val[:, 0:1], T.s16[:, 0:1]
     val = V(lambda: v.tensor_reduce(val16, T.p1[:, 0:8], AxisListType.X, MAX), mr)
     s16 = ts(s16a, val16, R16, R16, ADD, SUB, val)
@@ -168,13 +170,13 @@ def rank_program(g, core, T, topo):
     q1 = ts(T.rqt[:, 513:576:4], T.qrow[:], s16a, lo, EQ, MUL, s16)
     qrq = quant("rq", "rqt", 0, 144, 0, r0, r1, q0, q1)
     ml = mm(6, 128, "rq", 0, "rq", 16, True, True, qrq)
-    loff = V(lambda: v.tensor_copy(T.loff[:], T.p6[:, 112:128]), ml)
+    qsel = [ts(T.qm4[:, h:h + 1], T.pc[:, 8:9], 32.0 * h, None, EQ, None, pc) for h in range(4)]
+    loff = cp(T.loff[:], T.p6[:, 112:128], ml)
     sk, ss = pick("slot", 0, 256, "x", 128, "loff", 0, loff)
     send(lambda d: K("slot", 32 * d, 32 * d + 32).bitcast(dt.uint8), K("land", 32 * me, 32 * me + 32).bitcast(dt.uint8), "ra" if me < 4 else "rb", False, sk)
     send(lambda d: P("slot", 32 * d, 32 * d + 32), P("land", 32 * me, 32 * me + 32), "ra" if me < 4 else "rb", False, ss)
     lk, ls = pick("land", 32 * me, 32 * me + 32, "x", 128, "loff", 2 * me, loff)
 
-    qsel = [ts(T.qm4[:, h:h + 1], T.pc[:, 8:9], 32.0 * h, None, EQ, None, pc) for h in range(4)]
     qoff = ts(T.qoff[:], T.pc[:, 8:12], 4.0, None, MUL, None, pc)
 
     def books(i, load):
@@ -189,22 +191,22 @@ def rank_program(g, core, T, topo):
     bk1 = books(1, db1)
     qe = quant("e", "et", 0, 512, 0, *ed)
     qb1 = quant("b1", "bt1", 0, 512, 0, *bk1)
-    en = S(lambda: sc.activation(T.en[:], T.et[:], COPY, scale=-1.0), *ed)
+    en = [S((lambda b: lambda: sc.activation(T.en[:, 512 * b + b:512 * b + 512:4], T.ident[:], COPY, scale=-1.0))(b), gid, enm) for b in range(4)]
     mz = [fill(T[n][:], 0.0) for n in ("m1", "m2")]
     bk2 = books(2, db2)
-    qne = quant("ne", "en", 0, 512, 0, en)
+    qne = quant("ne", "en", 0, 512, 0, *en)
     qb2 = quant("b2", "bt2", 0, 512, 0, *bk2)
 
     def level(lev, z, book, banks, zdeps, bdeps, between):
         L = str(lev)
         n, m, t, td, tt, off, rm, sg = ["%s%s" % (a, L) for a in ("n", "m", "t", "td", "tt", "off", "rm", "sg")]
-        mmx = [mm(banks[i], 512, z, 128 * i, book, 0, True, True, bdeps, *zdeps[i]) for i in (0, 1)]
-        between(mmx)
+        mmx = {(i, j): mm(banks[2 * i + j], 256, z, 128 * i, book, 256 * j, True, True, bdeps, *zdeps[i]) for i in (0, 1) for j in (0, 1)}
+        between()
         scan, sign = {}, {}
         for i in (0, 1):
             for h in range(4):
-                c = 512 * i + 128 * h
-                scan[i, h] = V((lambda i, h, c: lambda: v.tensor_tensor_scan(T[rm][:, c:c + 128], T.neg[:], T["p%d" % banks[i]][:, 128 * h:128 * h + 128], LOW, MAX, MAX))(i, h, c), mmx[i], neg)
+                c, b, o = 512 * i + 128 * h, "p%d" % banks[2 * i + h // 2], 128 * (h % 2)
+                scan[i, h] = V((lambda c, b, o: lambda: v.tensor_tensor_scan(T[rm][:, c:c + 128], T.neg[:], T[b][:, o:o + 128], LOW, MAX, MAX))(c, b, o), mmx[i, h // 2], neg)
         for i in (0, 1):
             for h in range(4):
                 c = 512 * i + 128 * h
@@ -213,37 +215,30 @@ def rank_program(g, core, T, topo):
         for h in range(4):
             for a in range(4):
                 o, w, dep = T[m][32 * h:32 * h + 32, a:8:4], T[n][32 * a:32 * a + 32, 2 * h:2 * h + 2], (sign[0, h], sign[1, h], mz[lev - 1])
-                if 4 * h + a < 10:
-                    mv.append(V((lambda o, w: lambda: v.tensor_copy(o, w))(o, w), *dep))
-                else:
-                    mv.append(act(o, w, *dep))
+                mv.append((cp if 4 * h + a < 10 else act)(o, w, *dep))
         tr = V(lambda: v.transpose(T[t][:], T[m][:]), *mv)
         dup = []
         for a in (0, 1):
             for u in (0, 1):
                 o, w = T[td][:, 32 * a + 16 * u:32 * a + 16 * u + 16], T[t][:, 16 * a:16 * a + 16]
-                if u == 0:
-                    dup.append(V((lambda o, w: lambda: v.tensor_copy(o, w))(o, w), tr))
-                else:
-                    dup.append(act(o, w, tr))
+                dup.append((cp if u == 0 else act)(o, w, tr))
         tr2 = V(lambda: v.transpose(T[tt][:], T[td][:]), *dup)
         of = [ts(T[off][:, a:16:2], T[tt][:, 32 * a:32 * a + 8], T.qoff[:, 0:1], None, ADD, None, tr2, qoff) for a in (0, 1)]
-        dn = [D("y", "dn" + L, T["ws" + L][:, 32 * h:32 * h + 32, 0], T[t][32 * h:32 * h + 8, 0:32], tr) for h in range(4)]
         do = [D("y", "do" + L, T["wl" + L][me:me + 1, 32 * h:32 * h + 32, 0], T[t][32 * h + me:32 * h + me + 1, 0:32], tr) for h in range(4)]
-        return scan, of, dn, do
+        return scan, of, mv, tr, do
 
     arr = [arrivals("ra", range(0, 4), 2, False), arrivals("rb", range(4, 8), 2, False)]
     zd = [[arr[i]] + ([lk, ls] if me // 4 == i else []) for i in (0, 1)]
     bank = {}
 
-    def unpack(mmx):
+    def unpack():
         for b in range(4):
             bank[0, b] = (2 + b, mm(2 + b, 128, "e", 128 * b, "land", 0, True, False, qe, *zd[0]))
-        for b in (0, 1):
-            bank[1, b] = (6 + b, mm(6 + b, 128, "e", 128 * b, "land", 128, True, False, qe, loff, *zd[1]))
-    scan1, of1, dn1, do1 = level(1, "land", "b1", (0, 1), zd, qb1, unpack)
-    for b in (2, 3):
-        bank[1, b] = (b - 2, mm(b - 2, 128, "e", 128 * b, "land", 128, True, False, *[scan1[b - 2, h] for h in range(4)]))
+    scan1, of1, mv1, tr1, do1 = level(1, "land", "b1", (0, 1, 6, 7), zd, [qb1, loff][0], unpack)
+    for b in range(4):
+        n = (0, 1, 6, 7)[b]
+        bank[1, b] = (n, mm(n, 128, "e", 128 * b, "land", 128, True, False, *[scan1[b // 2, 2 * (b % 2) + h] for h in (0, 1)]))
+    dn1 = [D("y", "dn1", T.ws1[:, 32 * h:32 * h + 32, 0], T.t1[32 * h:32 * h + 8, 0:32], tr1) for h in range(4)]
     va = [pick("va", 128 * i, 128 * i + 128, "b1", 512, "off1", 8 * i, *of1) for i in (0, 1)]
     send(lambda d: K("va", 32 * d, 32 * d + 32).bitcast(dt.uint8), K("hva", 32 * me, 32 * me + 32).bitcast(dt.uint8), "rva", False, va[0][0], va[1][0])
     send(lambda d: P("va", 32 * d, 32 * d + 32), P("hva", 32 * me, 32 * me + 32), "rva", False, va[0][1], va[1][1])
@@ -252,19 +247,18 @@ def rank_program(g, core, T, topo):
     for i in (0, 1):
         fin = [mm(bank[i, b][0], 128, "ne", 128 * b, "va", 128 * i, False, True, qne, *va[i]) for b in range(4)]
         for b in range(4):
-            o, w = T.rt[:, 512 * i + b:512 * i + 512:4], T["p%d" % bank[i, b][0]][:, 0:128]
-            if b % 2 == 0:
-                rc[i, b] = V((lambda o, w: lambda: v.tensor_copy(o, w))(o, w), fin[b])
-            else:
-                rc[i, b] = act(o, w, fin[b])
+            rc[i, b] = (cp if b % 2 == 0 else act)(T.rt[:, 512 * i + b:512 * i + 512:4], T["p%d" % bank[i, b][0]][:, 0:128], fin[b])
         qr.append(quant("r", "rt", 128 * i, 128 * i + 128, 512 * i, *[rc[i, b] for b in range(4)]))
 
-    scan2, of2, dn2, do2 = level(2, "r", "b2", (2, 3), [[qr[0]], [qr[1]]], qb2, lambda mmx: None)
+    scan2, of2, mv2, tr2, do2 = level(2, "r", "b2", (2, 3, 4, 5), [[qr[0]], [qr[1]]], qb2, lambda: None)
+    send(lambda d: T.m2[:, d:d + 1], T.wl2[me], "rn2", False, *mv2)
     vb = [pick("vb", 128 * i, 128 * i + 128, "b2", 512, "off2", 8 * i, *of2) for i in (0, 1)]
     send(lambda d: K("vb", 32 * d, 32 * d + 32).bitcast(dt.uint8), K("hvb", 32 * me, 32 * me + 32).bitcast(dt.uint8), "rvb", False, vb[0][0], vb[1][0])
-    send(lambda d: T.ws2[d], T.wl2[me], "rn2", True, *dn2)
     send(lambda d: P("vb", 32 * d, 32 * d + 32), P("hvb", 32 * me, 32 * me + 32), "rvb", False, vb[0][1], vb[1][1])
 
+    wrm = fill(T.wrow[:], -1.0)
+    fl = [D("y", "df%d" % i, T.wrow[4 * i - 4 + h:4 * i - 3 + h, 0:256], T["wl%d" % i][:, 32 * h:32 * h + 32, 0], arrivals("rn%d" % i, range(8), 1, i == 1), wrm, *do)
+          for i, do in ((1, do1), (2, do2)) for h in range(4)]
     ka, sa = pick("hva", 32 * me, 32 * me + 32, "b1", 512, "off1", 2 * me, *of1)
     kb, sb = pick("hvb", 32 * me, 32 * me + 32, "b2", 512, "off2", 2 * me, *of2)
     ha, hb, hk, hr, hrr = T.ha[:, 0:1], T.hb[:, 0:1], T.hk[:, 0:1], T.hr[:, 0:1], T.hrr[:, 0:1]
@@ -285,31 +279,24 @@ def rank_program(g, core, T, topo):
     h9 = ts(T.ht[:, 1:32:4], T.mask8[:], hrr, None, MUL, None, h6, mk, htm)
     h8 = ts(T.ht[:, 0:32:4], T.mask8[:], hb, None, MUL, None, h7, mk, htm)
     qh = quant("h", "ht", 0, 128, 0, h8, h9)
-    mh = mm(5, 128, "c", 0, "h", 0, True, True, qc, qh, rc[0, 3])
-    wrm = fill(T.wrow[:], -1.0)
+    mh = mm(5, 128, "c", 0, "h", 0, True, True, qc, qh, scan2[1, 2], scan2[1, 3])
     qz = [quant(n, "zt", 256, 384, 0, ztm) for n in ("hva", "hvb")]
     qw = quant("w", "wt", 0, 128, 0, dw)
-    hoff = V(lambda: v.tensor_copy(T.hoff[:], T.p5[:, 0:8]), mh)
-
-    def flat(lev, do):
-        L = str(lev)
-        return [D("y", "df" + L, T.wrow[4 * lev - 4 + h:4 * lev - 3 + h, 0:256], T["wl" + L][:, 32 * h:32 * h + 32, 0], arrivals("rn" + L, range(8), 1, True), wrm, *do) for h in range(4)]
+    hoff = cp(T.hoff[:], T.p5[:, 0:8], mh)
 
     oa = pick("oa", 0, 128, "hva", 384, "hoff", 0, hoff, qz[0], ka, sa, arrivals("rva", range(8), 2, False))
-    y1 = mm(4, 128, "w", 0, "oa", 0, True, False, qw, rc[0, 2], *oa)
+    y1 = mm(4, 128, "w", 0, "oa", 0, True, False, qw, scan2[1, 0], scan2[1, 1], *oa)
     D("y", "dst", T.oc[:, 0:512], K("oa", 0, 128).bitcast(dt.uint8), oa[0])
     for k in range(4):
         D("y", "dst", T.osc[4 * k:4 * k + 4, 0:128], T.s_oa[32 * k:32 * k + 4, :], oa[1])
-    f1 = flat(1, do1)
-    f2 = flat(2, do2)
     ob = pick("ob", 0, 128, "hvb", 384, "hoff", 0, hoff, qz[1], kb, sb, arrivals("rvb", range(8), 2, False))
     y2 = mm(4, 128, "w", 0, "ob", 0, False, True, *ob)
     D("s", "dso", T.oc[:, 512:1024], K("ob", 0, 128).bitcast(dt.uint8), ob[0])
     for k in range(4):
         D("s", "dso", T.osc[4 * k:4 * k + 4, 128:256], T.s_ob[32 * k:32 * k + 4, :], ob[1])
-    yc = V(lambda: v.tensor_copy(T.yt[:], T.p4[:, 0:128]), y2)
+    yc = cp(T.yt[:], T.p4[:, 0:128], y2)
     D("s", "dso", T.y[:], T.yt[:], yc)
-    wn = V(lambda: v.tensor_copy(T.wnf[:], T.wrow[:].indirect(T.hoff[:])), hoff, *f1, *f2)
+    wn = cp(T.wnf[:], T.wrow[:].indirect(T.hoff[:]), hoff, *fl)
     D("y", "dst", T.wn[:], T.wnf[0:8, :], wn)
 
     total, at = {}, []

@@ -5,42 +5,43 @@ BF, F32, I32, U16, COD, PL = "bfloat16", "float32", "int32", "uint16", "float8_e
 SCRATCH = {
     "xt": ("sbuf", [128, 512], BF), "cot": ("sbuf", [128, 512], BF), "wt": ("sbuf", [128, 512], BF),
     "br1": ("sbuf", [128, 512], BF), "br2": ("sbuf", [128, 512], BF), "bt1": ("sbuf", [128, 2048], BF), "bt2": ("sbuf", [128, 2048], BF),
-    "et": ("sbuf", [128, 2048], BF), "en": ("sbuf", [128, 2048], BF),
+    "et": ("sbuf", [128, 2048], BF), "en": ("sbuf", [128, 1536], BF), "st": ("sbuf", [128, 512], BF),
     "trt": ("sbuf", [128, 512], BF), "ct": ("sbuf", [128, 512], BF), "mt": ("sbuf", [128, 512], BF),
     "rqt": ("sbuf", [128, 576], BF), "ht": ("sbuf", [128, 512], BF), "zt": ("sbuf", [128, 512], BF),
     "rt": ("sbuf", [128, 1024], BF),
-    "ones": ("sbuf", [128, 128], BF), "ident": ("sbuf", [128, 128], BF), "tri": ("sbuf", [128, 128], BF),
-    "neg": ("sbuf", [128, 128], F32), "c75": ("sbuf", [128, 8], BF), "c128": ("sbuf", [128, 8], BF),
-    "rj": ("sbuf", [128, 128], BF), "ri": ("sbuf", [128, 128], BF), "qrow": ("sbuf", [128, 16], F32), "nrow": ("sbuf", [128, 16], F32),
-    "crow": ("sbuf", [128, 8], F32), "pi": ("sbuf", [128, 4], I32), "pj": ("sbuf", [128, 16], I32), "qm4": ("sbuf", [128, 4], F32),
-    "pc": ("sbuf", [128, 16], F32), "lo75": ("sbuf", [128, 4], F32), "qoff": ("sbuf", [128, 4], F32), "mask8": ("sbuf", [128, 8], F32),
+    "jd": ("sbuf", [128, 128], BF), "dg": ("sbuf", [128, 128], BF), "tri": ("sbuf", [128, 128], BF),
+    "low": ("sbuf", [128, 8], F32), "rs": ("sbuf", [128, 256], F32), "ri0": ("sbuf", [128, 32], BF), "ri": ("sbuf", [128, 256], BF),
+    "qrow": ("sbuf", [128, 16], F32), "nrow": ("sbuf", [128, 16], F32), "crow": ("sbuf", [128, 8], F32), "qm4": ("sbuf", [128, 4], F32),
+    "pm": ("sbuf", [128, 4], F32), "ph": ("sbuf", [128, 4], F32), "pl": ("sbuf", [128, 4], F32), "pr": ("sbuf", [128, 4], F32), "pq": ("sbuf", [128, 4], F32),
+    "lo75": ("sbuf", [128, 4], F32), "qoff": ("sbuf", [128, 4], F32), "mask8": ("sbuf", [128, 8], F32),
     "rmc": ("sbuf", [128, 8], F32), "val": ("sbuf", [128, 4], F32), "s16": ("sbuf", [128, 4], F32),
-    "qone": ("sbuf", [128, 16], F32), "qa": ("sbuf", [128, 16], F32), "ha": ("sbuf", [128, 4], F32), "hb": ("sbuf", [128, 4], F32),
+    "qone": ("sbuf", [128, 16], F32), "qa": ("sbuf", [128, 16], F32), "qj": ("sbuf", [128, 16], F32), "qk": ("sbuf", [128, 16], F32),
+    "ha": ("sbuf", [128, 4], F32), "hb": ("sbuf", [128, 4], F32),
     "hk": ("sbuf", [128, 4], F32), "hr": ("sbuf", [128, 4], F32), "hrr": ("sbuf", [128, 4], F32),
     "loff": ("sbuf", [128, 16], U16), "hoff": ("sbuf", [128, 8], U16),
     "rm1": ("sbuf", [128, 1024], F32), "rm2": ("sbuf", [128, 1024], F32), "sg1": ("sbuf", [128, 1024], BF), "sg2": ("sbuf", [128, 1024], BF),
     "n1": ("sbuf", [128, 8], F32), "n2": ("sbuf", [128, 8], F32), "m1": ("sbuf", [128, 32], BF), "m2": ("sbuf", [128, 32], BF),
-    "t1": ("sbuf", [128, 32], BF), "t2": ("sbuf", [128, 32], BF), "td1": ("sbuf", [128, 64], BF), "td2": ("sbuf", [128, 64], BF),
+    "td1": ("sbuf", [128, 64], BF), "td2": ("sbuf", [128, 64], BF),
     "tt1": ("sbuf", [128, 64], BF), "tt2": ("sbuf", [128, 64], BF), "off1": ("sbuf", [128, 16], U16), "off2": ("sbuf", [128, 16], U16),
     "ws1": ("dram", [8, 128, 1], BF), "wl1": ("dram", [8, 128, 1], BF), "wl2": ("dram", [8, 128, 1], BF),
     "wrow": ("sbuf", [128, 272], BF), "wnf": ("sbuf", [128, 128], F32), "yt": ("sbuf", [128, 128], F32),
 }
-for _n, _w in (("x", 128), ("co", 128), ("w", 128), ("b1", 512), ("b2", 512), ("e", 512), ("ne", 512), ("tr", 128), ("c", 128),
+for _n, _w in (("x", 128), ("co", 128), ("w", 128), ("b1", 512), ("b2", 512), ("e", 512), ("ne", 384), ("st", 128), ("n3", 128), ("tr", 128), ("c", 128),
                ("m", 128), ("rq", 144), ("h", 128), ("slot", 256), ("land", 256), ("va", 256), ("r", 256), ("vb", 256),
-               ("hva", 384), ("hvb", 384), ("oa", 128), ("ob", 128)):
+               ("hva", 272), ("hvb", 272), ("oa", 128), ("ob", 128)):
     SCRATCH["k_" + _n] = ("sbuf", [128, _w], COD)
     SCRATCH["s_" + _n] = ("sbuf", [128, _w], PL)
 for _n in range(8):
     SCRATCH["p%d" % _n] = ("psum", [128, 512], F32)
 SEMAPHORES = ["cv", "cs", "ce", "cg", "dx", "dco", "db1", "db2", "dw", "dn1", "do1", "do2", "df1", "df2", "dst", "dso",
-              "ra", "rb", "rva", "rvb", "rn1", "rn2", "loc"]
+              "ra", "rb", "rva", "rvb", "rn1", "rn2", "rs", "dn3", "dz", "loc"]
 
 ADD, SUB, MUL, MAX = AluOpType.add, AluOpType.subtract, AluOpType.mult, AluOpType.max
-GE, EQ, NE = AluOpType.is_ge, AluOpType.is_equal, AluOpType.not_equal
-AND = AluOpType.bitwise_and
+MIN, GE, EQ, NE = AluOpType.min, AluOpType.is_ge, AluOpType.is_equal, AluOpType.not_equal
 COPY, SIGN = ActivationFunctionType.Copy, ActivationFunctionType.Sign
 LOW = -1e29
-R16 = 1.5 * 2.0 ** 27
+BIG = 1e29
+R16, R32 = 1.5 * 2.0 ** 27, 1.5 * 2.0 ** 28
 
 
 def rank_program(g, core, T, topo):
@@ -117,96 +118,111 @@ def rank_program(g, core, T, topo):
     db2 = D("y", "db2", T.br2[:], T.b2[:])
     dw = D("y", "dw", T.wt[:], T.w[:])
 
-    ones = fill(T.ones[:], 1.0)
-    cot = fill(T.cot[:, 32:512], 0.0)
-    ztm = fill(T.zt[:], 0.0)
-    mtm = fill(T.mt[:], 0.0)
-    c75 = fill(T.c75[:], -7.5)
-    neg = fill(T.neg[:], LOW)
-    enm = fill(T.en[:], 0.0)
-
     def affine(out, in_, step, n, op, f, base, cm, *deps): return G(lambda: g.affine_select(out, in_, [[step, n]], op, f, base, cm), *deps)
     def iota(out, pattern, base, cm): return G(lambda: g.iota(out, pattern, base, cm, allow_small_or_imprecise_dtypes=True))
-    ga = affine(T.tri[:], T.ones[:], 1, 128, GE, 0.0, 0, -1, ones)
-    g2 = affine(T.trt[:, 2:512:4], T.ones[:], 0, 128, EQ, 0.0, 0, 1, ones)
-    g0 = affine(T.trt[:, 0:512:4], T.tri[:], 1, 128, NE, 1024.0, 0, -1, ga)
-    g3 = affine(T.trt[:, 3:512:4], T.ones[:], 0, 128, EQ, 0.0, -1, 1, ones)
-    gi = iota(T.c128[:], [[128, 8]], 0, 0)
-    gp = G(lambda: g.iota(T.pi[:], [[0, 4]], 0, 1))
-    gm2 = affine(T.mt[:, 2:32:4], T.c128[:], 0, 8, EQ, 0.0, 0, 1, gi, mtm)
-    gm3 = affine(T.mt[:, 3:32:4], T.c75[:], 0, 8, EQ, 0.0, -1, 1, c75, mtm)
-    gr0 = iota(T.rj[:], [[0, 8], [1, 16]], 0, 0)
-    gq = iota(T.qrow[:], [[128, 8], [16, 2]], 1024, 0)
-    gid = affine(T.ident[:], T.ones[:], 1, 128, EQ, 0.0, 0, -1, ones)
-    gn = iota(T.nrow[:], [[1, 16]], -16, 0)
-    gc = iota(T.crow[:], [[16, 8]], 0, 0)
+    def smul(out, in_, c, *deps): return S(lambda: sc.activation(out, in_, COPY, scale=c), *deps)
 
-    srq = act(T.rqt[:, 0:512], T.zt[:], ztm)
-    srq2 = act(T.rqt[:, 512:576], T.zt[:, 0:64], ztm)
-    s1 = S(lambda: sc.activation(T.trt[:, 1:512:4], T.trt[:, 0:512:4], COPY, scale=-1.0), g0)
-    gr = S(lambda: sc.activation(T.ri[:], T.rj[:], COPY, bias=-7.5), gr0)
-    ez = [act(T.et[:, 512 * b:512 * b + 512], T.zt[:], ztm) for b in range(4)]
-    ed = [act(T.et[:, 512 * b + b:512 * b + 512:4], T.ident[:], gid, ez[b]) for b in range(4)]
+    gj = iota(T.jd[:], [[1, 128]], 0, -1)
+    gr = iota(T.ri0[:], [[2, 16], [0, 2]], -15, 0)
+    gq = iota(T.qrow[:], [[256, 8], [32, 2]], 2048, 0)
+    ztm = fill(T.zt[:], 0.0)
+    stm = fill(T.st[:], 0.0)
+    sh = ts(T.st[:, 3:64:4], T.jd[:, 16 * me:16 * me + 16], 0.0, -1.0, EQ, MUL, gj, stm)
+    qst = quant("st", "st", 0, 128, 0, sh)
+    send(lambda d: K("st", 0, 16).bitcast(dt.uint8), K("n3", 16 * me, 16 * me + 16).bitcast(dt.uint8), "rs", False, qst)
+    send(lambda d: P("st", 0, 16), P("n3", 16 * me, 16 * me + 16), "rs", False)
 
-    qco = quant("co", "cot", 0, 128, 0, cot, dco)
+    def neg(b): return affine(T.en[:, 512 * b:512 * b + 512], T.zt[:], 1, 512, NE, -1.0, -b, -4, ztm)
+    en = [neg(0)]
+    own3 = [D("y", "dn3", K("n3", 16 * me, 16 * me + 16).bitcast(dt.uint8), K("st", 0, 16).bitcast(dt.uint8), qst),
+            D("y", "dn3", P("n3", 16 * me, 16 * me + 16), P("st", 0, 16), qst)]
+    dg = ts(T.dg[:], T.jd[:], 0.0, 2048.0, EQ, MUL, gj)
+    tri = ts(T.tri[:], T.jd[:], 0.0, 2.0, GE, MUL)
+    tr1s = fill(T.trt[:, 1:512:2], 1.0)
+    t0 = V(lambda: v.tensor_tensor(T.trt[:, 0:512:4], T.dg[:], T.tri[:], MAX), dg, tri)
+    low = fill(T.low[:], LOW)
+
+    coz = act(T.cot[:, 32:512], T.zt[:, 0:480], ztm)
+    rr = [act(T.ri[:, 0:32], T.ri0[:], gr)]
+    for n in (32, 64, 128):
+        rr.append((lambda n: act(T.ri[:, n:2 * n], T.ri[:, 0:n], rr[-1]))(n))
+    t2 = smul(T.trt[:, 2:512:4], T.trt[:, 0:512:4], -1.0, t0)
+    mtz = act(T.mt[:], T.zt[:])
+    rqz = act(T.rqt[:, 1:576:2], T.zt[:, 0:288])
+    ez = [act(T.et[:, 512 * b:512 * b + 512], T.zt[:]) for b in range(4)]
+
+    qco = quant("co", "cot", 0, 128, 0, dco, coz)
     qx = quant("x", "xt", 0, 128, 0, dx)
+    zc = [D("y", "dz", o, i, qco) for n in ("hva", "hvb") for o, i in ((K(n, 256, 272).bitcast(dt.uint8), K("co", 16, 32).bitcast(dt.uint8)), (P(n, 256, 272), P("co", 16, 32)))]
     ms = mm(0, 128, "x", 0, "co", 0, True, True, qco, qx)
-    qtr = quant("tr", "trt", 0, 128, 0, g0, s1, g2, g3)
-    rmc = V(lambda: v.tensor_tensor_scan(T.rmc[:], T.neg[:, 0:8], T.p0[:, 0:8], LOW, MAX, MAX), ms, neg)
-    ge0 = ts(T.mt[:, 0:32:4], T.rmc[:], T.rmc[:, 7:8], None, GE, None, rmc, mtm)
-    ge1 = ts(T.mt[:, 5:32:4], T.rmc[:, 0:7], T.rmc[:, 7:8], None, GE, None, rmc, mtm)
-    qm = quant("m", "mt", 0, 128, 0, ge0, ge1, gm2, gm3)
+    qtr = quant("tr", "trt", 0, 128, 0, t0, tr1s, t2)
+    m1c = ts(T.mt[0:1, 1:32:4], T.qrow[0:1, 0:16:2], -2048.0, None, ADD, None, gq, mtz)
+    m3c = fill(T.mt[32:33, 3:32:4], -15.0)
+    rmc = V(lambda: v.tensor_tensor_scan(T.rmc[:], T.low[:], T.p0[:, 0:8], LOW, MAX, MAX), ms, low)
+    ge0 = ts(T.mt[:, 0:32:4], T.rmc[:], T.rmc[:, 7:8], None, GE, None, rmc, mtz)
+    ge1 = ts(T.mt[:, 6:32:4], T.rmc[:, 0:7], T.rmc[:, 7:8], None, GE, None, rmc)
+    qm = quant("m", "mt", 0, 128, 0, ge0, ge1, m1c, m3c)
     mr = mm(1, 128, "tr", 0, "m", 0, True, True, qm, qtr)
-    pa = ts(T.pj[:, 0:4], T.pi[:], 112, None, AND, None, gp)
-    pb = ts(T.pj[:, 4:8], T.pi[:], 15, None, AND, None, gp)
-    pq = ts(T.pj[:, 8:12], T.pi[:], 96, None, AND, None, gp)
-    pc = cp(T.pc[:, 0:12], T.pj[:, 0:12], pa, pb, pq)
-    hi16, lo, val16, s16a = T.pc[:, 0:1], T.pc[:, 4:5], T.val[:, 0:1], T.s16[:, 0:1]
+    hi16, lo, val16, s16a = T.ph[:, 0:1], T.pl[:, 0:1], T.val[:, 0:1], T.s16[:, 0:1]
+    pm = ts(T.pm[:, 0:1], T.jd[:, 0:1], -1.0, -7.5, MUL, ADD)
+    pr = ts(T.pr[:, 0:1], T.jd[:, 0:1], -1.0, -15.5, MUL, ADD)
+    ph = ts(hi16, T.pm[:, 0:1], R16, R16, ADD, SUB, pm)
+    pq = ts(T.pq[:, 0:1], T.pr[:, 0:1], R32, R32, ADD, SUB, pr)
+    pl = ts(lo, T.pm[:, 0:1], hi16, 7.5, SUB, ADD, ph)
     val = V(lambda: v.tensor_reduce(val16, T.p1[:, 0:8], AxisListType.X, MAX), mr)
-    s16 = ts(s16a, val16, R16, R16, ADD, SUB, val)
-    r0 = ts(T.rqt[:, 0:512:4], T.ri[:], s16a, val16, ADD, EQ, s16, gr, srq)
-    r1 = ts(T.rqt[:, 1:512:4], T.ri[:], s16a, val16, ADD, EQ, s16)
-    q0 = ts(T.rqt[:, 512:576:4], T.qrow[:], s16a, hi16, EQ, MUL, gq, srq2, pc)
-    q1 = ts(T.rqt[:, 513:576:4], T.qrow[:], s16a, lo, EQ, MUL, s16)
-    qrq = quant("rq", "rqt", 0, 144, 0, r0, r1, q0, q1)
+    s16 = ts(s16a, val16, R32, R32, ADD, SUB, val)
+    r0 = ts(T.rqt[:, 0:512:2], T.ri[:], s16a, val16, ADD, EQ, s16, rr[-1], rqz)
+    q0 = ts(T.rqt[:, 512:576:4], T.qrow[:], s16a, hi16, EQ, MUL, gq, ph)
+    q1 = ts(T.rqt[:, 514:576:4], T.qrow[:], s16a, lo, EQ, MUL, pl)
+    qrq = quant("rq", "rqt", 0, 144, 0, r0, q0, q1)
     ml = mm(6, 128, "rq", 0, "rq", 16, True, True, qrq)
-    qsel = [ts(T.qm4[:, h:h + 1], T.pc[:, 8:9], 32.0 * h, None, EQ, None, pc) for h in range(4)]
+    qsel = [ts(T.qm4[:, h:h + 1], T.pq[:, 0:1], 32.0 * h, None, EQ, None, pq) for h in range(4)]
     loff = cp(T.loff[:], T.p6[:, 112:128], ml)
     sk, ss = pick("slot", 0, 256, "x", 128, "loff", 0, loff)
     send(lambda d: K("slot", 32 * d, 32 * d + 32).bitcast(dt.uint8), K("land", 32 * me, 32 * me + 32).bitcast(dt.uint8), "ra" if me < 4 else "rb", False, sk)
     send(lambda d: P("slot", 32 * d, 32 * d + 32), P("land", 32 * me, 32 * me + 32), "ra" if me < 4 else "rb", False, ss)
     lk, ls = pick("land", 32 * me, 32 * me + 32, "x", 128, "loff", 2 * me, loff)
+    ed = [smul(T.et[:, 512 * b + b:512 * b + 512:4], T.dg[:], 2.0 ** -11, dg, ez[b]) for b in range(4)]
+    en += [neg(b) for b in (1, 2)]
+    gn = iota(T.nrow[:], [[1, 16]], -16, 0)
+    gc = iota(T.crow[:], [[16, 8]], 0, 0)
+    htm = iota(T.ht[:], [[0, 512]], 0, 0)
+    h1 = ts(T.qone[:], T.qrow[:], s16a, None, EQ, None, s16)
+    h5 = ts(T.hr[:, 0:1], val16, s16a, 15.0, SUB, ADD, s16)
 
-    qoff = ts(T.qoff[:], T.pc[:, 8:12], 4.0, None, MUL, None, pc)
-
-    def books(i, load):
+    def books(i, load, onv):
         o = []
         for h in range(4):
             t, r, m = T["bt%d" % i][:, 512 * h:512 * h + 512], T["br%d" % i][:], T.qm4[:, h:h + 1]
-            if h < 2:
+            if h < onv:
                 o.append(ts(t, r, m, None, MUL, None, qsel[h], load))
             else:
-                o.append(S((lambda t, r, m: lambda: sc.activation(t, r, COPY, scale=m))(t, r, m), qsel[h], load))
+                o.append(smul(t, r, m, qsel[h], load))
         return o
-    bk1 = books(1, db1)
-    qe = quant("e", "et", 0, 512, 0, *ed)
-    qb1 = quant("b1", "bt1", 0, 512, 0, *bk1)
-    en = [S((lambda b: lambda: sc.activation(T.en[:, 512 * b + b:512 * b + 512:4], T.ident[:], COPY, scale=-1.0))(b), gid, enm) for b in range(4)]
+    bk1 = books(1, db1, 2)
+    qoff = ts(T.qoff[:, 0:1], T.pq[:, 0:1], 4.0, None, MUL, None, pq)
+    rs0 = fill(T.rs[:], BIG)
     mz = [fill(T[n][:], 0.0) for n in ("m1", "m2")]
-    bk2 = books(2, db2)
-    qne = quant("ne", "en", 0, 512, 0, *en)
-    qb2 = quant("b2", "bt2", 0, 512, 0, *bk2)
+    qe = quant("e", "et", 0, 512, 0, *ed)
+    rs = V(lambda: v.memset(T.rs[:, 0:256:128], LOW), rs0)
+    qb1 = quant("b1", "bt1", 0, 512, 0, *bk1)
+    bk2 = books(2, db2, 1)
+    qne = [quant("ne", "en", 0, 256, 0, en[0], en[1]), quant("ne", "en", 256, 384, 1024, en[2])]
 
-    def level(lev, z, book, banks, zdeps, bdeps, between):
+    def level(lev, z, book, banks, zdeps, bdeps, between, behind):
         L = str(lev)
-        n, m, t, td, tt, off, rm, sg = ["%s%s" % (a, L) for a in ("n", "m", "t", "td", "tt", "off", "rm", "sg")]
-        mmx = {(i, j): mm(banks[2 * i + j], 256, z, 128 * i, book, 256 * j, True, True, bdeps, *zdeps[i]) for i in (0, 1) for j in (0, 1)}
+        n, m, td, tt, off, rm, sg = ["%s%s" % (a, L) for a in ("n", "m", "td", "tt", "off", "rm", "sg")]
+        mmx = {(i, j): mm(banks[2 * i + j], 256, z, 128 * i, book, 256 * j, True, True, bdeps[j], *zdeps[i]) for i in (0, 1) for j in (0, 1)}
         between()
         scan, sign = {}, {}
         for i in (0, 1):
-            for h in range(4):
-                c, b, o = 512 * i + 128 * h, "p%d" % banks[2 * i + h // 2], 128 * (h % 2)
-                scan[i, h] = V((lambda c, b, o: lambda: v.tensor_tensor_scan(T[rm][:, c:c + 128], T.neg[:], T[b][:, o:o + 128], LOW, MAX, MAX))(c, b, o), mmx[i, h // 2], neg)
+            for j in (0, 1):
+                b = "p%d" % banks[2 * i + j]
+                for o, w in (((0, 128), (128, 128)) if i == 0 and j == 0 else ((0, 256),)):
+                    c = 512 * i + 256 * j + o
+                    h = V((lambda c, b, o, w: lambda: v.tensor_tensor_scan(T[rm][:, c:c + w], T.rs[:, 0:w], T[b][:, o:o + w], LOW, MIN, MAX))(c, b, o, w), mmx[i, j], rs)
+                    for k in range(o // 128, (o + w) // 128):
+                        scan[i, 2 * j + k] = h
         for i in (0, 1):
             for h in range(4):
                 c = 512 * i + 128 * h
@@ -215,88 +231,91 @@ def rank_program(g, core, T, topo):
         for h in range(4):
             for a in range(4):
                 o, w, dep = T[m][32 * h:32 * h + 32, a:8:4], T[n][32 * a:32 * a + 32, 2 * h:2 * h + 2], (sign[0, h], sign[1, h], mz[lev - 1])
-                mv.append((cp if 4 * h + a < 10 else act)(o, w, *dep))
-        tr = V(lambda: v.transpose(T[t][:], T[m][:]), *mv)
-        dup = []
-        for a in (0, 1):
-            for u in (0, 1):
-                o, w = T[td][:, 32 * a + 16 * u:32 * a + 16 * u + 16], T[t][:, 16 * a:16 * a + 16]
-                dup.append((cp if u == 0 else act)(o, w, tr))
+                mv.append((cp if 4 * h + a < NV else act)(o, w, *dep))
+        behind()
+        tr = V(lambda: v.transpose(T[td][:, 16:48], T[m][:]), *mv)
+        dup = [cp(T[td][:, 0:16], T[td][:, 16:32], tr), cp(T[td][:, 48:64], T[td][:, 32:48], tr)]
         tr2 = V(lambda: v.transpose(T[tt][:], T[td][:]), *dup)
         of = [ts(T[off][:, a:16:2], T[tt][:, 32 * a:32 * a + 8], T.qoff[:, 0:1], None, ADD, None, tr2, qoff) for a in (0, 1)]
-        do = [D("y", "do" + L, T["wl" + L][me:me + 1, 32 * h:32 * h + 32, 0], T[t][32 * h + me:32 * h + me + 1, 0:32], tr) for h in range(4)]
+        do = [D("y", "do" + L, T["wl" + L][me:me + 1, 32 * h:32 * h + 32, 0], T[td][32 * h + me:32 * h + me + 1, 16:48], tr) for h in range(4)]
         return scan, of, mv, tr, do
 
+    NV = 11
     arr = [arrivals("ra", range(0, 4), 2, False), arrivals("rb", range(4, 8), 2, False)]
     zd = [[arr[i]] + ([lk, ls] if me // 4 == i else []) for i in (0, 1)]
-    bank = {}
+    bank, late = {}, {}
+    ha, hb, hk, hr, hrr = T.ha[:, 0:1], T.hb[:, 0:1], T.hk[:, 0:1], T.hr[:, 0:1], T.hrr[:, 0:1]
+
+    def behind1():
+        mk = ts(T.mask8[:], T.crow[:], hi16, None, EQ, None, ph, gc)
+        h2 = V(lambda: v.tensor_tensor(T.qa[:], T.qone[:], T.nrow[:], MUL), h1, gn)
+        h4 = S(lambda: sc.activation(T.qj[:], T.qone[:], COPY, accum_out=hk), h1)
+        h3 = S(lambda: sc.activation(T.qk[:], T.qa[:], COPY, accum_out=ha), h2)
+        h6 = S(lambda: sc.activation(hrr, hr, COPY, scale=hk), h5, h4)
+        h7 = S(lambda: sc.activation(hb, ha, COPY, bias=16.0), h3)
+        late["h"] = [S(lambda: sc.activation(T.ht[:, 1:32:4], T.mask8[:], COPY, scale=hrr), h6, mk, htm),
+                     S(lambda: sc.activation(T.ht[:, 0:32:4], T.mask8[:], COPY, scale=hb), h7, mk, htm)]
 
     def unpack():
         for b in range(4):
             bank[0, b] = (2 + b, mm(2 + b, 128, "e", 128 * b, "land", 0, True, False, qe, *zd[0]))
-    scan1, of1, mv1, tr1, do1 = level(1, "land", "b1", (0, 1, 6, 7), zd, [qb1, loff][0], unpack)
+    scan1, of1, mv1, tr1, do1 = level(1, "land", "b1", (0, 1, 6, 7), zd, (qb1, qb1), unpack, behind1)
     for b in range(4):
         n = (0, 1, 6, 7)[b]
         bank[1, b] = (n, mm(n, 128, "e", 128 * b, "land", 128, True, False, *[scan1[b // 2, 2 * (b % 2) + h] for h in (0, 1)]))
-    dn1 = [D("y", "dn1", T.ws1[:, 32 * h:32 * h + 32, 0], T.t1[32 * h:32 * h + 8, 0:32], tr1) for h in range(4)]
+    dn1 = [D("y", "dn1", T.ws1[:, 32 * h:32 * h + 32, 0], T.td1[32 * h:32 * h + 8, 16:48], tr1) for h in range(4)]
     va = [pick("va", 128 * i, 128 * i + 128, "b1", 512, "off1", 8 * i, *of1) for i in (0, 1)]
     send(lambda d: K("va", 32 * d, 32 * d + 32).bitcast(dt.uint8), K("hva", 32 * me, 32 * me + 32).bitcast(dt.uint8), "rva", False, va[0][0], va[1][0])
     send(lambda d: P("va", 32 * d, 32 * d + 32), P("hva", 32 * me, 32 * me + 32), "rva", False, va[0][1], va[1][1])
     send(lambda d: T.ws1[d], T.wl1[me], "rn1", True, *dn1)
+    ctm = iota(T.ct[:], [[0, 512]], 0, 0)
     qr, rc = [], {}
+    third = arrivals("rs", range(8), 2, False)
+
+    def book2(k): return quant("b2", "bt2", 256 * k, 256 * k + 256, 1024 * k, *bk2[2 * k:2 * k + 2])
+    qb2 = [book2(0)]
     for i in (0, 1):
-        fin = [mm(bank[i, b][0], 128, "ne", 128 * b, "va", 128 * i, False, True, qne, *va[i]) for b in range(4)]
+        fin = [mm(bank[i, b][0], 128, *(("ne", 128 * b) if b < 3 else ("n3", 0)), "va", 128 * i, False, True, qne[b // 2] if b < 3 else qne[1], *(va[i] + ((third, own3[0], own3[1]) if b == 3 else ()))) for b in range(4)]
         for b in range(4):
             rc[i, b] = (cp if b % 2 == 0 else act)(T.rt[:, 512 * i + b:512 * i + 512:4], T["p%d" % bank[i, b][0]][:, 0:128], fin[b])
         qr.append(quant("r", "rt", 128 * i, 128 * i + 128, 512 * i, *[rc[i, b] for b in range(4)]))
+        if i == 0:
+            qb2.append(book2(1))
 
-    scan2, of2, mv2, tr2, do2 = level(2, "r", "b2", (2, 3, 4, 5), [[qr[0]], [qr[1]]], qb2, lambda: None)
+    def behind2():
+        late["wr"] = S(lambda: sc.activation(T.wrow[:], T.zt[:, 0:272], COPY, bias=-1.0))
+    scan2, of2, mv2, tr2, do2 = level(2, "r", "b2", (2, 3, 4, 5), [[qr[0]], [qr[1]]], qb2, lambda: None, behind2)
     send(lambda d: T.m2[:, d:d + 1], T.wl2[me], "rn2", False, *mv2)
     vb = [pick("vb", 128 * i, 128 * i + 128, "b2", 512, "off2", 8 * i, *of2) for i in (0, 1)]
     send(lambda d: K("vb", 32 * d, 32 * d + 32).bitcast(dt.uint8), K("hvb", 32 * me, 32 * me + 32).bitcast(dt.uint8), "rvb", False, vb[0][0], vb[1][0])
     send(lambda d: P("vb", 32 * d, 32 * d + 32), P("hvb", 32 * me, 32 * me + 32), "rvb", False, vb[0][1], vb[1][1])
 
-    wrm = fill(T.wrow[:], -1.0)
-    fl = [D("y", "df%d" % i, T.wrow[4 * i - 4 + h:4 * i - 3 + h, 0:256], T["wl%d" % i][:, 32 * h:32 * h + 32, 0], arrivals("rn%d" % i, range(8), 1, i == 1), wrm, *do)
+    fl = [D("y", "df%d" % i, T.wrow[4 * i - 4 + h:4 * i - 3 + h, 0:256], T["wl%d" % i][:, 32 * h:32 * h + 32, 0], arrivals("rn%d" % i, range(8), 1, i == 1), late["wr"], *do)
           for i, do in ((1, do1), (2, do2)) for h in range(4)]
+    l75 = S(lambda: sc.activation(T.lo75[:, 0:1], lo, COPY, bias=-15.0, scale=2.0), pl)
+    c0 = ts(T.ct[:, 0:512:4], T.ri[:, 0:256:2], T.lo75[:, 0:1], 16.0, EQ, MUL, l75, ctm, rr[-1])
+    c1 = ts(T.ct[:, 1:512:4], T.ri[:, 0:256:2], T.lo75[:, 0:1], 0.5, EQ, MUL, l75)
+    qh = quant("h", "ht", 0, 128, 0, *late["h"])
+    qc = quant("c", "ct", 0, 128, 0, c0, c1)
+    mh = mm(5, 128, "c", 0, "h", 0, True, True, qc, qh, scan2[1, 2], scan2[1, 3])
+    qw = quant("w", "wt", 0, 128, 0, dw)
     ka, sa = pick("hva", 32 * me, 32 * me + 32, "b1", 512, "off1", 2 * me, *of1)
     kb, sb = pick("hvb", 32 * me, 32 * me + 32, "b2", 512, "off2", 2 * me, *of2)
-    ha, hb, hk, hr, hrr = T.ha[:, 0:1], T.hb[:, 0:1], T.hk[:, 0:1], T.hr[:, 0:1], T.hrr[:, 0:1]
-    h1 = ts(T.qone[:], T.qrow[:], s16a, None, EQ, None, s16)
-    l75 = ts(T.lo75[:, 0:1], lo, -7.5, None, ADD, None, pc)
-    ctm = fill(T.ct[:], 0.0)
-    htm = fill(T.ht[:], 0.0)
-    h5 = ts(hr, val16, s16a, 7.5, SUB, ADD, s16)
-    mk = ts(T.mask8[:], T.crow[:], hi16, None, EQ, None, pc, gc)
-    h2 = V(lambda: v.tensor_tensor(T.qa[:], T.qone[:], T.nrow[:], MUL), h1, gn)
-    h4 = V(lambda: v.tensor_reduce(hk, T.qone[:], AxisListType.X, ADD), h1)
-    c0 = ts(T.ct[:, 0:512:4], T.ri[:], T.lo75[:, 0:1], 16.0, EQ, MUL, l75, ctm, gr)
-    c1 = ts(T.ct[:, 1:512:4], T.ri[:], T.lo75[:, 0:1], None, EQ, None, l75)
-    h3 = V(lambda: v.tensor_reduce(ha, T.qa[:], AxisListType.X, ADD), h2)
-    h6 = V(lambda: v.tensor_tensor(hrr, hr, hk, MUL), h5, h4)
-    qc = quant("c", "ct", 0, 128, 0, c0, c1)
-    h7 = ts(hb, ha, 16.0, None, ADD, None, h3)
-    h9 = ts(T.ht[:, 1:32:4], T.mask8[:], hrr, None, MUL, None, h6, mk, htm)
-    h8 = ts(T.ht[:, 0:32:4], T.mask8[:], hb, None, MUL, None, h7, mk, htm)
-    qh = quant("h", "ht", 0, 128, 0, h8, h9)
-    mh = mm(5, 128, "c", 0, "h", 0, True, True, qc, qh, scan2[1, 2], scan2[1, 3])
-    qz = [quant(n, "zt", 256, 384, 0, ztm) for n in ("hva", "hvb")]
-    qw = quant("w", "wt", 0, 128, 0, dw)
     hoff = cp(T.hoff[:], T.p5[:, 0:8], mh)
 
-    oa = pick("oa", 0, 128, "hva", 384, "hoff", 0, hoff, qz[0], ka, sa, arrivals("rva", range(8), 2, False))
+    oa = pick("oa", 0, 128, "hva", 272, "hoff", 0, hoff, zc[0], zc[1], ka, sa, arrivals("rva", range(8), 2, False))
     y1 = mm(4, 128, "w", 0, "oa", 0, True, False, qw, scan2[1, 0], scan2[1, 1], *oa)
     D("y", "dst", T.oc[:, 0:512], K("oa", 0, 128).bitcast(dt.uint8), oa[0])
     for k in range(4):
         D("y", "dst", T.osc[4 * k:4 * k + 4, 0:128], T.s_oa[32 * k:32 * k + 4, :], oa[1])
-    ob = pick("ob", 0, 128, "hvb", 384, "hoff", 0, hoff, qz[1], kb, sb, arrivals("rvb", range(8), 2, False))
+    ob = pick("ob", 0, 128, "hvb", 272, "hoff", 0, hoff, zc[2], zc[3], kb, sb, arrivals("rvb", range(8), 2, False))
     y2 = mm(4, 128, "w", 0, "ob", 0, False, True, *ob)
-    D("s", "dso", T.oc[:, 512:1024], K("ob", 0, 128).bitcast(dt.uint8), ob[0])
+    wn = act(T.wnf[:], T.wrow[:].indirect(T.hoff[:]), hoff, *fl)
+    D("y", "dst", T.oc[:, 512:1024], K("ob", 0, 128).bitcast(dt.uint8), ob[0])
     for k in range(4):
-        D("s", "dso", T.osc[4 * k:4 * k + 4, 128:256], T.s_ob[32 * k:32 * k + 4, :], ob[1])
+        D("y", "dst", T.osc[4 * k:4 * k + 4, 128:256], T.s_ob[32 * k:32 * k + 4, :], ob[1])
     yc = cp(T.yt[:], T.p4[:, 0:128], y2)
     D("s", "dso", T.y[:], T.yt[:], yc)
-    wn = cp(T.wnf[:], T.wrow[:].indirect(T.hoff[:]), hoff, *fl)
     D("y", "dst", T.wn[:], T.wnf[0:8, :], wn)
 
     total, at = {}, []

from concourse.bass import DstId, RemoteDMATransfer
from concourse.mybir import dt, AluOpType, AxisListType, ActivationFunctionType

BF, F32, I32, U16, COD, PL = "bfloat16", "float32", "int32", "uint16", "float8_e4m3fn_x4", "uint8"
SCRATCH = {
    "xt": ("sbuf", [128, 512], BF), "cot": ("sbuf", [128, 512], BF), "wt": ("sbuf", [128, 512], BF),
    "br1": ("sbuf", [128, 512], BF), "br2": ("sbuf", [128, 512], BF), "bt1": ("sbuf", [128, 2048], BF), "bt2": ("sbuf", [128, 2048], BF),
    "et": ("sbuf", [128, 2048], BF), "en": ("sbuf", [128, 1536], BF), "st": ("sbuf", [128, 512], BF),
    "trt": ("sbuf", [128, 512], BF), "ct": ("sbuf", [128, 512], BF), "mt": ("sbuf", [128, 512], BF),
    "rqt": ("sbuf", [128, 576], BF), "ht": ("sbuf", [128, 512], BF), "zt": ("sbuf", [128, 512], BF),
    "rt": ("sbuf", [128, 1024], BF),
    "jd": ("sbuf", [128, 128], BF), "dg": ("sbuf", [128, 128], BF), "tri": ("sbuf", [128, 128], BF),
    "low": ("sbuf", [128, 8], F32), "rs": ("sbuf", [128, 256], F32), "ri0": ("sbuf", [128, 32], BF), "ri": ("sbuf", [128, 256], BF),
    "qrow": ("sbuf", [128, 16], F32), "nrow": ("sbuf", [128, 16], F32), "crow": ("sbuf", [128, 8], F32), "qm4": ("sbuf", [128, 4], F32),
    "pm": ("sbuf", [128, 4], F32), "ph": ("sbuf", [128, 4], F32), "pl": ("sbuf", [128, 4], F32), "pr": ("sbuf", [128, 4], F32), "pq": ("sbuf", [128, 4], F32),
    "lo75": ("sbuf", [128, 4], F32), "qoff": ("sbuf", [128, 4], F32), "mask8": ("sbuf", [128, 8], F32),
    "rmc": ("sbuf", [128, 8], F32), "val": ("sbuf", [128, 4], F32), "s16": ("sbuf", [128, 4], F32),
    "qone": ("sbuf", [128, 16], F32), "qa": ("sbuf", [128, 16], F32), "qj": ("sbuf", [128, 16], F32), "qk": ("sbuf", [128, 16], F32),
    "ha": ("sbuf", [128, 4], F32), "hb": ("sbuf", [128, 4], F32),
    "hk": ("sbuf", [128, 4], F32), "hr": ("sbuf", [128, 4], F32), "hrr": ("sbuf", [128, 4], F32),
    "loff": ("sbuf", [128, 16], U16), "hoff": ("sbuf", [128, 8], U16),
    "rm1": ("sbuf", [128, 1024], F32), "rm2": ("sbuf", [128, 1024], F32), "sg1": ("sbuf", [128, 1024], BF), "sg2": ("sbuf", [128, 1024], BF),
    "n1": ("sbuf", [128, 8], F32), "n2": ("sbuf", [128, 8], F32), "m1": ("sbuf", [128, 32], BF), "m2": ("sbuf", [128, 32], BF),
    "td1": ("sbuf", [128, 64], BF), "td2": ("sbuf", [128, 64], BF),
    "tt1": ("sbuf", [128, 64], BF), "tt2": ("sbuf", [128, 64], BF), "off1": ("sbuf", [128, 16], U16), "off2": ("sbuf", [128, 16], U16),
    "ws1": ("dram", [8, 128, 1], BF), "wl1": ("dram", [8, 128, 1], BF), "wl2": ("dram", [8, 128, 1], BF),
    "wrow": ("sbuf", [128, 272], BF), "wnf": ("sbuf", [128, 128], F32), "yt": ("sbuf", [128, 128], F32),
}
for _n, _w in (("x", 128), ("co", 128), ("w", 128), ("b1", 512), ("b2", 512), ("e", 512), ("ne", 384), ("st", 128), ("n3", 128), ("tr", 128), ("c", 128),
               ("m", 128), ("rq", 144), ("h", 128), ("slot", 256), ("land", 256), ("va", 256), ("r", 256), ("vb", 256),
               ("hva", 272), ("hvb", 272), ("oa", 128), ("ob", 128)):
    SCRATCH["k_" + _n] = ("sbuf", [128, _w], COD)
    SCRATCH["s_" + _n] = ("sbuf", [128, _w], PL)
for _n in range(8):
    SCRATCH["p%d" % _n] = ("psum", [128, 512], F32)
SEMAPHORES = ["cv", "cs", "ce", "cg", "dx", "dco", "db1", "db2", "dw", "dn1", "do1", "do2", "df1", "df2", "dst", "dso",
              "ra", "rb", "rva", "rvb", "rn1", "rn2", "rs", "dn3", "dz", "loc"]

ADD, SUB, MUL, MAX = AluOpType.add, AluOpType.subtract, AluOpType.mult, AluOpType.max
MIN, GE, EQ, NE = AluOpType.min, AluOpType.is_ge, AluOpType.is_equal, AluOpType.not_equal
COPY, SIGN = ActivationFunctionType.Copy, ActivationFunctionType.Sign
LOW = -1e29
BIG = 1e29
R16, R32 = 1.5 * 2.0 ** 27, 1.5 * 2.0 ** 28


def rank_program(g, core, T, topo):
    me = T.rank_of(core)
    if me is None:
        return
    ops, queue = [], {"v": g.vector, "s": g.scalar, "e": g.tensor, "g": g, "y": g.sync}
    own_sem = {"v": "cv", "s": "cs", "e": "ce", "g": "cg"}

    def add(q, fn, deps=(), sem=None, inc=1):
        ops.append((q, fn, list(deps), own_sem[q] if sem is None else sem, inc))
        return len(ops) - 1

    def V(fn, *deps): return add("v", fn, deps)
    def S(fn, *deps): return add("s", fn, deps)
    def E(fn, *deps): return add("e", fn, deps)
    def G(fn, *deps): return add("g", fn, deps)
    def D(q, sem, out, in_, *deps): return add(q, lambda: queue[q].dma_start(out, in_), deps, sem, 16)

    v, sc, te = g.vector, g.scalar, g.tensor
    K = lambda n, a, b: T["k_" + n][:, a:b]
    P = lambda n, a, b: T["s_" + n][:, a:b]

    def ts(out, in0, s1, s2, op0, op1, *deps):
        return V(lambda: v.tensor_scalar(out, in0, s1, s2, op0) if op1 is None else v.tensor_scalar(out, in0, s1, s2, op0, op1), *deps)

    def cp(out, in_, *deps): return V(lambda: v.tensor_copy(out, in_), *deps)

    def act(out, in_, *deps): return S(lambda: sc.activation(out, in_, COPY), *deps)

    def fill(ap, c): return V(lambda: v.memset(ap, c))

    def quant(n, tile, a, b, src, *deps):
        return V(lambda: v.quantize_mx(K(n, a, b), P(n, a, b), T[tile][:, src:src + 4 * (b - a)]), *deps)

    def mm(bank, n, w, wa, x, xa, start, stop, *deps):
        return E(lambda: te.matmul_mx(T["p%d" % bank][:, 0:n], K(w, wa, wa + 128), P(w, wa, wa + 128), K(x, xa, xa + n), P(x, xa, xa + n), start, stop), *deps)

    def pick(o, a, b, w, wn, off, c, *deps):
        k = (b - a) // 16
        return (V(lambda: v.tensor_copy(K(o, a, b).bitcast(dt.uint32), K(w, 0, wn).bitcast(dt.uint32).indirect(T[off][:, c:c + k])), *deps),
                S(lambda: sc.activation(P(o, a, b), P(w, 0, wn).indirect(T[off][:, c:c + k]), COPY), *deps))

    others = [d for d in range(len(T.cores)) if d != me]
    far = [d for d in others if topo.die(T.cores[d]) != topo.die(core)]
    near = [d for d in others if d not in far]
    eng = {}
    for part, k in ((far, 0), (near, 1)):
        for i, d in enumerate(part):
            e = topo.engines(core, T.cores[d])[k::2]
            w = len(e) // 4
            eng[d] = e[w * i:w * i + w]
    expect = {}

    def send(src, dst, sem, one, *deps):
        def call():
            tr = []
            for d in far + near:
                rid, pid, _ = topo.addr(T.cores[d])
                m = sum(1 << e for e in (eng[d][:1] if one else eng[d]))
                tr.append(RemoteDMATransfer(dst_ids=[DstId(rid=rid, pnc=pid)], dma_engine_mask=m, remote_sem=T.sem[sem], src=src(d), dst=dst))
            return g.remote_dma_fused(tr, local_sem=T.sem["loc"])
        for d in others:
            expect["loc"] = expect.get("loc", 0) + (1 if one else len(eng[d]))
        return add("g", call, deps, "")

    def arrivals(sem, ranks, n, one):
        expect[sem] = n * sum(1 if one else len(topo.engines(T.cores[s], core)) // 8 for s in ranks if s != me)
        return (sem, expect[sem])

    dco = D("s", "dco", T.cot[:, 0:32], T.co[:, 0:32])
    dx = D("y", "dx", T.xt[:], T.x[:])
    db1 = D("y", "db1", T.br1[:], T.b1[:])
    db2 = D("y", "db2", T.br2[:], T.b2[:])
    dw = D("y", "dw", T.wt[:], T.w[:])

    def affine(out, in_, step, n, op, f, base, cm, *deps): return G(lambda: g.affine_select(out, in_, [[step, n]], op, f, base, cm), *deps)
    def iota(out, pattern, base, cm): return G(lambda: g.iota(out, pattern, base, cm, allow_small_or_imprecise_dtypes=True))
    def smul(out, in_, c, *deps): return S(lambda: sc.activation(out, in_, COPY, scale=c), *deps)

    gj = iota(T.jd[:], [[1, 128]], 0, -1)
    gr = iota(T.ri0[:], [[2, 16], [0, 2]], -15, 0)
    gq = iota(T.qrow[:], [[256, 8], [32, 2]], 2048, 0)
    ztm = fill(T.zt[:], 0.0)
    stm = fill(T.st[:], 0.0)
    sh = ts(T.st[:, 3:64:4], T.jd[:, 16 * me:16 * me + 16], 0.0, -1.0, EQ, MUL, gj, stm)
    qst = quant("st", "st", 0, 128, 0, sh)
    send(lambda d: K("st", 0, 16).bitcast(dt.uint8), K("n3", 16 * me, 16 * me + 16).bitcast(dt.uint8), "rs", False, qst)
    send(lambda d: P("st", 0, 16), P("n3", 16 * me, 16 * me + 16), "rs", False)

    def neg(b): return affine(T.en[:, 512 * b:512 * b + 512], T.zt[:], 1, 512, NE, -1.0, -b, -4, ztm)
    en = [neg(0)]
    own3 = [D("y", "dn3", K("n3", 16 * me, 16 * me + 16).bitcast(dt.uint8), K("st", 0, 16).bitcast(dt.uint8), qst),
            D("y", "dn3", P("n3", 16 * me, 16 * me + 16), P("st", 0, 16), qst)]
    dg = ts(T.dg[:], T.jd[:], 0.0, 2048.0, EQ, MUL, gj)
    tri = ts(T.tri[:], T.jd[:], 0.0, 2.0, GE, MUL)
    tr1s = fill(T.trt[:, 1:512:2], 1.0)
    t0 = V(lambda: v.tensor_tensor(T.trt[:, 0:512:4], T.dg[:], T.tri[:], MAX), dg, tri)
    low = fill(T.low[:], LOW)

    coz = act(T.cot[:, 32:512], T.zt[:, 0:480], ztm)
    rr = [act(T.ri[:, 0:32], T.ri0[:], gr)]
    for n in (32, 64, 128):
        rr.append((lambda n: act(T.ri[:, n:2 * n], T.ri[:, 0:n], rr[-1]))(n))
    t2 = smul(T.trt[:, 2:512:4], T.trt[:, 0:512:4], -1.0, t0)
    mtz = act(T.mt[:], T.zt[:])
    rqz = act(T.rqt[:, 1:576:2], T.zt[:, 0:288])
    ez = [act(T.et[:, 512 * b:512 * b + 512], T.zt[:]) for b in range(4)]

    qco = quant("co", "cot", 0, 128, 0, dco, coz)
    qx = quant("x", "xt", 0, 128, 0, dx)
    zc = [D("y", "dz", o, i, qco) for n in ("hva", "hvb") for o, i in ((K(n, 256, 272).bitcast(dt.uint8), K("co", 16, 32).bitcast(dt.uint8)), (P(n, 256, 272), P("co", 16, 32)))]
    ms = mm(0, 128, "x", 0, "co", 0, True, True, qco, qx)
    qtr = quant("tr", "trt", 0, 128, 0, t0, tr1s, t2)
    m1c = ts(T.mt[0:1, 1:32:4], T.qrow[0:1, 0:16:2], -2048.0, None, ADD, None, gq, mtz)
    m3c = fill(T.mt[32:33, 3:32:4], -15.0)
    rmc = V(lambda: v.tensor_tensor_scan(T.rmc[:], T.low[:], T.p0[:, 0:8], LOW, MAX, MAX), ms, low)
    ge0 = ts(T.mt[:, 0:32:4], T.rmc[:], T.rmc[:, 7:8], None, GE, None, rmc, mtz)
    ge1 = ts(T.mt[:, 6:32:4], T.rmc[:, 0:7], T.rmc[:, 7:8], None, GE, None, rmc)
    qm = quant("m", "mt", 0, 128, 0, ge0, ge1, m1c, m3c)
    mr = mm(1, 128, "tr", 0, "m", 0, True, True, qm, qtr)
    hi16, lo, val16, s16a = T.ph[:, 0:1], T.pl[:, 0:1], T.val[:, 0:1], T.s16[:, 0:1]
    pm = ts(T.pm[:, 0:1], T.jd[:, 0:1], -1.0, -7.5, MUL, ADD)
    pr = ts(T.pr[:, 0:1], T.jd[:, 0:1], -1.0, -15.5, MUL, ADD)
    ph = ts(hi16, T.pm[:, 0:1], R16, R16, ADD, SUB, pm)
    pq = ts(T.pq[:, 0:1], T.pr[:, 0:1], R32, R32, ADD, SUB, pr)
    pl = ts(lo, T.pm[:, 0:1], hi16, 7.5, SUB, ADD, ph)
    val = V(lambda: v.tensor_reduce(val16, T.p1[:, 0:8], AxisListType.X, MAX), mr)
    s16 = ts(s16a, val16, R32, R32, ADD, SUB, val)
    r0 = ts(T.rqt[:, 0:512:2], T.ri[:], s16a, val16, ADD, EQ, s16, rr[-1], rqz)
    q0 = ts(T.rqt[:, 512:576:4], T.qrow[:], s16a, hi16, EQ, MUL, gq, ph)
    q1 = ts(T.rqt[:, 514:576:4], T.qrow[:], s16a, lo, EQ, MUL, pl)
    qrq = quant("rq", "rqt", 0, 144, 0, r0, q0, q1)
    ml = mm(6, 128, "rq", 0, "rq", 16, True, True, qrq)
    qsel = [ts(T.qm4[:, h:h + 1], T.pq[:, 0:1], 32.0 * h, None, EQ, None, pq) for h in range(4)]
    loff = cp(T.loff[:], T.p6[:, 112:128], ml)
    sk, ss = pick("slot", 0, 256, "x", 128, "loff", 0, loff)
    send(lambda d: K("slot", 32 * d, 32 * d + 32).bitcast(dt.uint8), K("land", 32 * me, 32 * me + 32).bitcast(dt.uint8), "ra" if me < 4 else "rb", False, sk)
    send(lambda d: P("slot", 32 * d, 32 * d + 32), P("land", 32 * me, 32 * me + 32), "ra" if me < 4 else "rb", False, ss)
    lk, ls = pick("land", 32 * me, 32 * me + 32, "x", 128, "loff", 2 * me, loff)
    ed = [smul(T.et[:, 512 * b + b:512 * b + 512:4], T.dg[:], 2.0 ** -11, dg, ez[b]) for b in range(4)]
    en += [neg(b) for b in (1, 2)]
    gn = iota(T.nrow[:], [[1, 16]], -16, 0)
    gc = iota(T.crow[:], [[16, 8]], 0, 0)
    htm = iota(T.ht[:], [[0, 512]], 0, 0)
    h1 = ts(T.qone[:], T.qrow[:], s16a, None, EQ, None, s16)
    h5 = ts(T.hr[:, 0:1], val16, s16a, 15.0, SUB, ADD, s16)

    def books(i, load, onv):
        o = []
        for h in range(4):
            t, r, m = T["bt%d" % i][:, 512 * h:512 * h + 512], T["br%d" % i][:], T.qm4[:, h:h + 1]
            if h < onv:
                o.append(ts(t, r, m, None, MUL, None, qsel[h], load))
            else:
                o.append(smul(t, r, m, qsel[h], load))
        return o
    bk1 = books(1, db1, 2)
    qoff = ts(T.qoff[:, 0:1], T.pq[:, 0:1], 4.0, None, MUL, None, pq)
    rs0 = fill(T.rs[:], BIG)
    mz = [fill(T[n][:], 0.0) for n in ("m1", "m2")]
    qe = quant("e", "et", 0, 512, 0, *ed)
    rs = V(lambda: v.memset(T.rs[:, 0:256:128], LOW), rs0)
    qb1 = quant("b1", "bt1", 0, 512, 0, *bk1)
    bk2 = books(2, db2, 1)
    qne = [quant("ne", "en", 0, 256, 0, en[0], en[1]), quant("ne", "en", 256, 384, 1024, en[2])]

    def level(lev, z, book, banks, zdeps, bdeps, between, behind):
        L = str(lev)
        n, m, td, tt, off, rm, sg = ["%s%s" % (a, L) for a in ("n", "m", "td", "tt", "off", "rm", "sg")]
        mmx = {(i, j): mm(banks[2 * i + j], 256, z, 128 * i, book, 256 * j, True, True, bdeps[j], *zdeps[i]) for i in (0, 1) for j in (0, 1)}
        between()
        scan, sign = {}, {}
        for i in (0, 1):
            for j in (0, 1):
                b = "p%d" % banks[2 * i + j]
                for o, w in (((0, 128), (128, 128)) if i == 0 and j == 0 else ((0, 256),)):
                    c = 512 * i + 256 * j + o
                    h = V((lambda c, b, o, w: lambda: v.tensor_tensor_scan(T[rm][:, c:c + w], T.rs[:, 0:w], T[b][:, o:o + w], LOW, MIN, MAX))(c, b, o, w), mmx[i, j], rs)
                    for k in range(o // 128, (o + w) // 128):
                        scan[i, 2 * j + k] = h
        for i in (0, 1):
            for h in range(4):
                c = 512 * i + 128 * h
                sign[i, h] = S((lambda i, h, c: lambda: sc.activation(T[sg][:, c:c + 128], T[rm][:, c:c + 128], SIGN, bias=T[rm][:, c + 127:c + 128], scale=-1.0, accum_out=T[n][:, 2 * h + i:2 * h + i + 1]))(i, h, c), scan[i, h])
        mv = []
        for h in range(4):
            for a in range(4):
                o, w, dep = T[m][32 * h:32 * h + 32, a:8:4], T[n][32 * a:32 * a + 32, 2 * h:2 * h + 2], (sign[0, h], sign[1, h], mz[lev - 1])
                mv.append((cp if 4 * h + a < NV else act)(o, w, *dep))
        behind()
        tr = V(lambda: v.transpose(T[td][:, 16:48], T[m][:]), *mv)
        dup = [cp(T[td][:, 0:16], T[td][:, 16:32], tr), cp(T[td][:, 48:64], T[td][:, 32:48], tr)]
        tr2 = V(lambda: v.transpose(T[tt][:], T[td][:]), *dup)
        of = [ts(T[off][:, a:16:2], T[tt][:, 32 * a:32 * a + 8], T.qoff[:, 0:1], None, ADD, None, tr2, qoff) for a in (0, 1)]
        do = [D("y", "do" + L, T["wl" + L][me:me + 1, 32 * h:32 * h + 32, 0], T[td][32 * h + me:32 * h + me + 1, 16:48], tr) for h in range(4)]
        return scan, of, mv, tr, do

    NV = 11
    arr = [arrivals("ra", range(0, 4), 2, False), arrivals("rb", range(4, 8), 2, False)]
    zd = [[arr[i]] + ([lk, ls] if me // 4 == i else []) for i in (0, 1)]
    bank, late = {}, {}
    ha, hb, hk, hr, hrr = T.ha[:, 0:1], T.hb[:, 0:1], T.hk[:, 0:1], T.hr[:, 0:1], T.hrr[:, 0:1]

    def behind1():
        mk = ts(T.mask8[:], T.crow[:], hi16, None, EQ, None, ph, gc)
        h2 = V(lambda: v.tensor_tensor(T.qa[:], T.qone[:], T.nrow[:], MUL), h1, gn)
        h4 = S(lambda: sc.activation(T.qj[:], T.qone[:], COPY, accum_out=hk), h1)
        h3 = S(lambda: sc.activation(T.qk[:], T.qa[:], COPY, accum_out=ha), h2)
        h6 = S(lambda: sc.activation(hrr, hr, COPY, scale=hk), h5, h4)
        h7 = S(lambda: sc.activation(hb, ha, COPY, bias=16.0), h3)
        late["h"] = [S(lambda: sc.activation(T.ht[:, 1:32:4], T.mask8[:], COPY, scale=hrr), h6, mk, htm),
                     S(lambda: sc.activation(T.ht[:, 0:32:4], T.mask8[:], COPY, scale=hb), h7, mk, htm)]

    def unpack():
        for b in range(4):
            bank[0, b] = (2 + b, mm(2 + b, 128, "e", 128 * b, "land", 0, True, False, qe, *zd[0]))
    scan1, of1, mv1, tr1, do1 = level(1, "land", "b1", (0, 1, 6, 7), zd, (qb1, qb1), unpack, behind1)
    for b in range(4):
        n = (0, 1, 6, 7)[b]
        bank[1, b] = (n, mm(n, 128, "e", 128 * b, "land", 128, True, False, *[scan1[b // 2, 2 * (b % 2) + h] for h in (0, 1)]))
    dn1 = [D("y", "dn1", T.ws1[:, 32 * h:32 * h + 32, 0], T.td1[32 * h:32 * h + 8, 16:48], tr1) for h in range(4)]
    va = [pick("va", 128 * i, 128 * i + 128, "b1", 512, "off1", 8 * i, *of1) for i in (0, 1)]
    send(lambda d: K("va", 32 * d, 32 * d + 32).bitcast(dt.uint8), K("hva", 32 * me, 32 * me + 32).bitcast(dt.uint8), "rva", False, va[0][0], va[1][0])
    send(lambda d: P("va", 32 * d, 32 * d + 32), P("hva", 32 * me, 32 * me + 32), "rva", False, va[0][1], va[1][1])
    send(lambda d: T.ws1[d], T.wl1[me], "rn1", True, *dn1)
    ctm = iota(T.ct[:], [[0, 512]], 0, 0)
    qr, rc = [], {}
    third = arrivals("rs", range(8), 2, False)

    def book2(k): return quant("b2", "bt2", 256 * k, 256 * k + 256, 1024 * k, *bk2[2 * k:2 * k + 2])
    qb2 = [book2(0)]
    for i in (0, 1):
        fin = [mm(bank[i, b][0], 128, *(("ne", 128 * b) if b < 3 else ("n3", 0)), "va", 128 * i, False, True, qne[b // 2] if b < 3 else qne[1], *(va[i] + ((third, own3[0], own3[1]) if b == 3 else ()))) for b in range(4)]
        for b in range(4):
            rc[i, b] = (cp if b % 2 == 0 else act)(T.rt[:, 512 * i + b:512 * i + 512:4], T["p%d" % bank[i, b][0]][:, 0:128], fin[b])
        qr.append(quant("r", "rt", 128 * i, 128 * i + 128, 512 * i, *[rc[i, b] for b in range(4)]))
        if i == 0:
            qb2.append(book2(1))

    def behind2():
        late["wr"] = S(lambda: sc.activation(T.wrow[:], T.zt[:, 0:272], COPY, bias=-1.0))
    scan2, of2, mv2, tr2, do2 = level(2, "r", "b2", (2, 3, 4, 5), [[qr[0]], [qr[1]]], qb2, lambda: None, behind2)
    send(lambda d: T.m2[:, d:d + 1], T.wl2[me], "rn2", False, *mv2)
    vb = [pick("vb", 128 * i, 128 * i + 128, "b2", 512, "off2", 8 * i, *of2) for i in (0, 1)]
    send(lambda d: K("vb", 32 * d, 32 * d + 32).bitcast(dt.uint8), K("hvb", 32 * me, 32 * me + 32).bitcast(dt.uint8), "rvb", False, vb[0][0], vb[1][0])
    send(lambda d: P("vb", 32 * d, 32 * d + 32), P("hvb", 32 * me, 32 * me + 32), "rvb", False, vb[0][1], vb[1][1])

    fl = [D("y", "df%d" % i, T.wrow[4 * i - 4 + h:4 * i - 3 + h, 0:256], T["wl%d" % i][:, 32 * h:32 * h + 32, 0], arrivals("rn%d" % i, range(8), 1, i == 1), late["wr"], *do)
          for i, do in ((1, do1), (2, do2)) for h in range(4)]
    l75 = S(lambda: sc.activation(T.lo75[:, 0:1], lo, COPY, bias=-15.0, scale=2.0), pl)
    c0 = ts(T.ct[:, 0:512:4], T.ri[:, 0:256:2], T.lo75[:, 0:1], 16.0, EQ, MUL, l75, ctm, rr[-1])
    c1 = ts(T.ct[:, 1:512:4], T.ri[:, 0:256:2], T.lo75[:, 0:1], 0.5, EQ, MUL, l75)
    qh = quant("h", "ht", 0, 128, 0, *late["h"])
    qc = quant("c", "ct", 0, 128, 0, c0, c1)
    mh = mm(5, 128, "c", 0, "h", 0, True, True, qc, qh, scan2[1, 2], scan2[1, 3])
    qw = quant("w", "wt", 0, 128, 0, dw)
    ka, sa = pick("hva", 32 * me, 32 * me + 32, "b1", 512, "off1", 2 * me, *of1)
    kb, sb = pick("hvb", 32 * me, 32 * me + 32, "b2", 512, "off2", 2 * me, *of2)
    hoff = cp(T.hoff[:], T.p5[:, 0:8], mh)

    oa = pick("oa", 0, 128, "hva", 272, "hoff", 0, hoff, zc[0], zc[1], ka, sa, arrivals("rva", range(8), 2, False))
    y1 = mm(4, 128, "w", 0, "oa", 0, True, False, qw, scan2[1, 0], scan2[1, 1], *oa)
    D("y", "dst", T.oc[:, 0:512], K("oa", 0, 128).bitcast(dt.uint8), oa[0])
    for k in range(4):
        D("y", "dst", T.osc[4 * k:4 * k + 4, 0:128], T.s_oa[32 * k:32 * k + 4, :], oa[1])
    ob = pick("ob", 0, 128, "hvb", 272, "hoff", 0, hoff, zc[2], zc[3], kb, sb, arrivals("rvb", range(8), 2, False))
    y2 = mm(4, 128, "w", 0, "ob", 0, False, True, *ob)
    wn = act(T.wnf[:], T.wrow[:].indirect(T.hoff[:]), hoff, *fl)
    D("y", "dst", T.oc[:, 512:1024], K("ob", 0, 128).bitcast(dt.uint8), ob[0])
    for k in range(4):
        D("y", "dst", T.osc[4 * k:4 * k + 4, 128:256], T.s_ob[32 * k:32 * k + 4, :], ob[1])
    yc = cp(T.yt[:], T.p4[:, 0:128], y2)
    D("s", "dso", T.y[:], T.yt[:], yc)
    D("y", "dst", T.wn[:], T.wnf[0:8, :], wn)

    total, at = {}, []
    for q, fn, deps, sem, inc in ops:
        if sem:
            total[sem] = total.get(sem, 0) + inc
        at.append((sem, total.get(sem, 0)))
    total.update(expect)
    known, most = {q: {} for q in queue}, {}

    def wait(q, sem, n):
        if known[q].get(sem, 0) < n:
            queue[q].wait_ge(T.sem[sem], n)
            known[q][sem] = n
            most[sem] = max(most.get(sem, 0), n)
    for q, fn, deps, sem, inc in ops:
        need = {}
        for d in deps:
            s, n = d if isinstance(d, tuple) else at[d]
            if s.startswith("d"):
                n = total[s]
            need[s] = max(need.get(s, 0), n)
        for s in need:
            wait(q, s, need[s])
        ins = fn()
        if sem:
            ins.then_inc(T.sem[sem], inc)
    for s in total:
        if most.get(s, 0) < total[s]:
            wait("g", s, total[s])
